import numpy as np
import ml_dtypes


def mxq(x, axis, fmt="e4m3"):
    dtype, down = {"e4m3": (ml_dtypes.float8_e4m3fn, 7), "e5m2": (ml_dtypes.float8_e5m2, 14)}[fmt]
    v = np.moveaxis(np.asarray(x, np.float32).astype(ml_dtypes.bfloat16).astype(np.float64), axis, -1)
    blocks = v.reshape(v.shape[:-1] + (-1, 32))
    amax = np.abs(blocks).max(-1, keepdims=True)
    byte = np.maximum(np.where(amax > 0, np.frexp(amax)[1] - 1 + 127, 0) - down, 1)
    scale = np.exp2(byte - 127.0)
    codes = (blocks / scale).astype(np.float32).astype(dtype).astype(np.float64)
    return np.moveaxis((codes * scale).reshape(v.shape), -1, axis)


WIDE = False


def mx_kscale(k):
    if not WIDE:
        return np.ones(k)
    levels = np.array([10, -10, 5, -5, 0])
    if k % 512:
        return np.exp2(np.random.permutation(np.resize(levels, k // 32))).repeat(32)
    a = np.empty((k // 512, 16))
    for p in range(k // 512):
        a[p, :8] = np.random.permutation(np.resize(levels, 8))
        for g in range(8):
            far = levels[np.abs(levels - a[p, g]) >= 10]
            a[p, g + 8] = far[np.random.randint(len(far))]
    return np.exp2(a.ravel()).repeat(32)


def f64(x):
    return np.asarray(x).astype(np.float64)


def striped(idx):
    return np.tile(idx.reshape(-1, 16).T, (8, 1)).astype(np.uint16)


def unstriped(offs):
    return offs[:16].T.reshape(-1).astype(np.int64)


E2M1 = np.array([0.0, 0.5, 1.0, 1.5, 2.0, 3.0, 4.0, 6.0, -0.0, -0.5, -1.0, -1.5, -2.0, -3.0, -4.0, -6.0])


def pack_weight(w, fmt):
    k, n = w.shape
    w = f64(np.asarray(w, np.float32).astype(ml_dtypes.bfloat16)).reshape(k // 32, 32, n)
    amax = np.abs(w).max(1)
    if fmt == "e4m3":
        byte = np.frexp(amax)[1] - 1 + 127 - 7
    else:
        mant, ex = np.frexp(amax / 6.0)
        byte = np.where(mant > 0.5, ex, ex - 1) + 127
    byte = np.clip(np.where(amax > 0, byte, 1), 1, 254)
    scaled = (w * np.exp2(127.0 - byte)[:, None, :]).reshape(k, n).astype(np.float32)
    by_word = np.ascontiguousarray(scaled.reshape(k // 512, 128, 4, n).transpose(0, 1, 3, 2))
    if fmt == "e4m3":
        words = by_word.astype(ml_dtypes.float8_e4m3fn).view(np.uint8)
    else:
        c = by_word.astype(ml_dtypes.float4_e2m1fn).view(np.uint8) & 0xF
        words = (c[..., 0::2] | (c[..., 1::2] << 4)).reshape(k // 512, 128, 2 * n)
    return np.ascontiguousarray(words), np.ascontiguousarray(byte.astype(np.uint8).reshape(k // 512, 16, n))


def unpack_weight(words, scales, fmt):
    g, _, n = scales.shape
    words = np.ascontiguousarray(words).reshape(g, 128, n, -1)
    if fmt == "e4m3":
        vals = words.view(ml_dtypes.float8_e4m3fn).astype(np.float64)
    else:
        nib = np.empty((g, 128, n, 4), np.uint8)
        nib[..., 0::2] = words & 0xF
        nib[..., 1::2] = words >> 4
        vals = E2M1[nib]
    vals = vals * np.repeat(np.exp2(scales.astype(np.float64) - 127.0), 8, axis=1)[..., None]
    return vals.transpose(0, 1, 3, 2).reshape(g * 512, n)


def gelu(v):
    return 0.5 * v * (1.0 + np.tanh(np.sqrt(2.0 / np.pi) * (v + 0.044715 * v**3)))


def bf(x):
    return np.asarray(x, np.float32).astype(ml_dtypes.bfloat16)


def planes(Y):
    n, m = Y.shape
    b = f64(bf(Y)).reshape(n // 32, 32, m)
    amax = np.abs(b).max(1)
    byte = np.clip(np.where(amax > 0, np.frexp(amax)[1] - 1 + 127 - 7, 1), 1, 254)
    codes = (b * np.exp2(127.0 - byte)[:, None, :]).reshape(n, m).astype(np.float32).astype(ml_dtypes.float8_e4m3fn).view(np.uint8)
    words = codes.reshape(n // 512, 128, 4, m).transpose(0, 1, 3, 2)
    return np.ascontiguousarray(words), np.ascontiguousarray(byte.astype(np.uint8).reshape(n // 512, 16, m))


K, H, N, T, S = 1024, 1024, 512, 2048, 1024


def setup_inputs():
    n = np.random.standard_normal
    s = mx_kscale(K)[:, None]
    u = mx_kscale(H)[:, None]
    tab_words, tab_scales = pack_weight(n((K, T)) * s, "e4m3")
    offs = striped(np.random.permutation(T)[:S])
    w1 = (1.2 * n((K, H)) / np.sqrt(K) / s).astype(np.float32)
    w2 = (1.2 * np.exp(0.3 * n(H)) * u[:, 0]).astype(np.float32)
    w3_words, w3_scales = pack_weight(0.7 * n((K, H)) / np.sqrt(K) / s * u.T, "e2m1")
    w4_words, w4_scales = pack_weight(n((H, N)) / np.sqrt(H) / u, "e4m3")
    tpl = n((N, S)).astype(np.float32)
    return {"tab_words": tab_words, "tab_scales": tab_scales, "offs": offs,
            "w1": w1, "w2": w2, "w3_words": w3_words, "w3_scales": w3_scales,
            "w4_words": w4_words, "w4_scales": w4_scales, "tpl": tpl}


def reference(tab_words, tab_scales, offs, w1, w2, w3_words, w3_scales,
              w4_words, w4_scales, tpl):
    v = unpack_weight(tab_words, tab_scales, "e4m3")[:, unstriped(offs)]
    w3 = unpack_weight(w3_words, w3_scales, "e2m1")
    w4 = unpack_weight(w4_words, w4_scales, "e4m3")
    first = mxq(f64(w1), 0, "e4m3").T @ v
    skip = w3.T @ v
    h = f64(w2)[:, None] * np.tanh(first) + skip
    words, scales = planes(h)
    sig = w4.T @ mxq(h, 0, "e4m3")
    y = np.square(f64(tpl) - sig)
    return y, h, words, scales

@@ -1,0 +1,306 @@
+from contextlib import ExitStack
+
+import concourse.mybir as mybir
+
+K, H, N, T, S = 1024, 1024, 512, 2048, 1024
+FLOPS = 2 * (2 * K * H * S + H * N * S)
+
+F32 = mybir.dt.float32
+BF16 = mybir.dt.bfloat16
+I32 = mybir.dt.int32
+U32 = mybir.dt.uint32
+U16 = mybir.dt.uint16
+U8 = mybir.dt.uint8
+E4M3 = mybir.dt.float8_e4m3fn_x4
+E2M1 = mybir.dt.float4_e2m1fn_x4
+ACT = mybir.ActivationFunctionType
+ALU = mybir.AluOpType
+
+P = 128
+PACK = 4
+SPAN = P * PACK
+PASSES = K // SPAN
+GROUPS = H // SPAN
+CHUNK = 512
+CHUNKS = S // CHUNK
+QUADS = 4
+
+
+def tile_list_sonar_template_misfit_kernel(
+    tc, tab_words, tab_scales, offs, w1, w2, w3_words, w3_scales, w4_words, w4_scales, tpl,
+    out_0, out_1, out_2, out_3,
+):
+    nc = tc.nc
+    with ExitStack() as ctx:
+        keep = ctx.enter_context(tc.tile_pool(name="keep", bufs=1))
+        ring = ctx.enter_context(tc.tile_pool(name="ring", bufs=3))
+        stage = ctx.enter_context(tc.tile_pool(name="stage", bufs=1))
+        psum = ctx.enter_context(tc.psum_pool(name="psum", bufs=8))
+
+        def held(shape, dtype, name):
+            return keep.tile(shape, dtype, name=name, align_bytes=64)
+
+        offsets = keep.tile([P, S // 16], U16, name="offsets")
+        nc.sync.dma_start(offsets[:], offs)
+
+        tab_plane = held([P, T], U8, "tab_plane")
+        w3_plane_raw = held([P, PASSES, H], U8, "w3_plane_raw")
+        v_plane1 = held([P, S], U8, "v_plane1")
+        w4_plane = held([P, N], U8, "w4_plane")
+        warm = held([P, 1], F32, "warm")
+        warm_out = held([P, 1], F32, "warm_out")
+        nc.vector.memset(tab_plane[:].bitcast(I32), 0)
+        nc.vector.memset(warm[:], 0.0)
+        nc.vector.memset(v_plane1[:].bitcast(I32), 0)
+        nc.gpsimd.memset(w3_plane_raw[:].rearrange("p a n -> p (a n)").bitcast(I32), 0)
+        for q in range(QUADS):
+            nc.scalar.dma_start(
+                tab_plane[32 * q : 32 * q + 8, :].bitcast(I32),
+                tab_scales[:, 4 * q : 4 * q + 4, :].bitcast(I32))
+        nc.scalar.activation(warm_out[:], warm[:], ACT.Tanh)
+        for q in range(QUADS):
+            nc.gpsimd.dma_start(
+                w3_plane_raw[32 * q : 32 * q + 4].bitcast(I32),
+                w3_scales[:, 4 * q : 4 * q + 4, :].rearrange("a r n -> r a n").bitcast(I32))
+        gain = held([P, GROUPS, PACK], F32, "gain")
+        nc.gpsimd.dma_start(gain[:], w2.rearrange("(g p t) -> p g t", p=P, t=PACK))
+        nc.gpsimd.memset(w4_plane[:].bitcast(I32), 0)
+        for q in range(QUADS):
+            nc.gpsimd.dma_start(
+                w4_plane[32 * q : 32 * q + 8, :].bitcast(I32),
+                w4_scales[:, 4 * q : 4 * q + 4, :].bitcast(I32))
+
+        tab = {}
+
+        def load_tab(a):
+            tab[a] = held([P, T], I32, f"tab{a}")
+            nc.sync.dma_start(tab[a][:], tab_words[a].rearrange("p t i -> p (t i)").bitcast(I32))
+
+        w3_raw = stage.tile([P, PASSES, 2 * H // 4], I32, name="staged1")
+
+        w1_raw = {}
+
+        def load_w1(g, a, lo, hi):
+            if lo == 0:
+                w1_raw[g, a] = stage.tile([P, PACK, SPAN], F32, name=f"staged{a}")
+            rows = w1[SPAN * a : SPAN * (a + 1), SPAN * g + lo : SPAN * g + hi]
+            nc.sync.dma_start(w1_raw[g, a][:, :, lo:hi], rows.rearrange("(p i) c -> p i c", i=PACK))
+
+        template = []
+
+        def load_template(u):
+            rows = stage.tile([P, 2, S], F32, name=f"staged{u}")
+            nc.sync.dma_start(rows[:], tpl[2 * P * u : 2 * P * (u + 1), :].rearrange("(b p) j -> p b j", p=P))
+            template.append(rows)
+
+        nc.sync.dma_start(w3_raw[:], w3_words.rearrange("a p n -> p a n").bitcast(I32))
+        load_tab(0)
+        load_w1(0, 0, 0, SPAN)
+        load_tab(1)
+
+        v_plane0 = held([P, S], U8, "v_plane0")
+
+        def gather_planes():
+            nc.vector.tensor_copy(v_plane0[:], tab_plane[:].indirect(offsets[:]))
+            for q in range(QUADS):
+                nc.sync.dma_start(
+                    v_plane1[32 * q : 32 * q + 4, :].bitcast(I32),
+                    v_plane0[32 * q + 4 : 32 * q + 8, :].bitcast(I32))
+
+        v_plane = [v_plane0, v_plane1]
+        v = {}
+
+        def gather(a, c):
+            v[a, c] = held([P, CHUNK], U32, f"v{a}{c}")
+            cols = CHUNK // 16
+            nc.vector.tensor_copy(v[a, c][:], tab[a][:].bitcast(U32).indirect(offsets[:, cols * c : cols * (c + 1)]))
+
+        w3 = {}
+        w3_plane = {}
+
+        def deal_w3_words(g):
+            w3[g] = held([P, PASSES, 2 * SPAN], U8, f"w3_{g}")
+            nc.vector.tensor_copy(
+                w3[g][:].bitcast(U16).rearrange("p a (t m) -> p a t m", t=PACK),
+                w3_raw[:].bitcast(U16)[:, :, SPAN * g : SPAN * (g + 1)].rearrange("p a (m t) -> p a t m", t=PACK))
+
+        def deal_w3_plane(g):
+            w3_plane[g] = held([P, PASSES, SPAN], U8, f"w3_plane{g}")
+            nc.vector.tensor_copy(
+                w3_plane[g][:].rearrange("p a (t m) -> p a t m", t=PACK),
+                w3_plane_raw[:, :, SPAN * g : SPAN * (g + 1)].rearrange("p a (m t) -> p a t m", t=PACK))
+
+        w1_bf = {}
+
+        def round_w1(g, a, lo, hi, copy):
+            if lo == 0:
+                w1_bf[g, a] = held([P, SPAN * PACK], BF16, f"w1_bf{g}{a}")
+            dealt = w1_bf[g, a][:].rearrange("p (t m i) -> p m i t", t=PACK, i=PACK)
+            copy(dealt[:, lo // PACK : hi // PACK],
+                 w1_raw[g, a][:, :, lo:hi].rearrange("p i (m t) -> p m i t", t=PACK))
+
+        w1_codes = {}
+        w1_plane = {}
+
+        def quantize_w1(g, a):
+            w1_codes[g, a] = held([P, SPAN], U32, f"w1_codes{g}{a}")
+            w1_plane[g, a] = held([P, SPAN], U8, f"w1_plane{g}{a}")
+            nc.vector.quantize_mx(w1_codes[g, a][:].bitcast(E4M3), w1_plane[g, a][:], w1_bf[g, a][:])
+
+        def bank():
+            return psum.tile([P, CHUNK], F32, name="bank")
+
+        def first_pass(acc, g, c, t, a):
+            m = slice(P * t, P * (t + 1))
+            nc.tensor.matmul_mx(
+                acc[:], w1_codes[g, a][:, m].bitcast(E4M3), w1_plane[g, a][:, m],
+                v[a, c][:].bitcast(E4M3), v_plane0[4 * a : P, CHUNK * c : CHUNK * (c + 1)],
+                start=(a == 0), stop=(a == PASSES - 1))
+
+        def skip_pass(acc, g, c, t, a):
+            nc.tensor.matmul_mx(
+                acc[:], w3[g][:, a, 2 * P * t : 2 * P * (t + 1)].bitcast(E2M1), w3_plane[g][:, a, P * t : P * (t + 1)],
+                v[a, c][:].bitcast(E4M3), v_plane[a][:, CHUNK * c : CHUNK * (c + 1)],
+                start=(a == 0), stop=(a == PASSES - 1))
+
+        h = {}
+
+        def combine(g, c, t, first, skip):
+            if t == 0:
+                h[g, c] = held([P, PACK, CHUNK], F32, f"h{g}{c}")
+            th = ring.tile([P, CHUNK], F32, name="th")
+            nc.scalar.activation(th[:], first[:], ACT.Tanh)
+            nc.vector.scalar_tensor_tensor(h[g, c][:, t, :], th[:], gain[:, g, t : t + 1], skip[:], ALU.mult, ALU.add)
+            if t % 2 == 1:
+                rows = out_1[SPAN * g : SPAN * (g + 1), CHUNK * c : CHUNK * (c + 1)].rearrange("(p t) j -> p t j", t=PACK)
+                nc.sync.dma_start(rows[:, t - 1 : t + 1, :], h[g, c][:, t - 1 : t + 1, :])
+
+        def slice_of_h(g, c, t):
+            first, skip = bank(), bank()
+            for a in range(PASSES):
+                first_pass(first, g, c, t, a)
+            for a in range(PASSES):
+                skip_pass(skip, g, c, t, a)
+            combine(g, c, t, first, skip)
+
+        h_bf = {}
+
+        def round_h(g, c, on_vector):
+            h_bf[g, c] = held([P, CHUNK * PACK], BF16, f"h_bf{g}{c}")
+            dst = h_bf[g, c][:].rearrange("p (b i t) -> p b t i", i=4, t=PACK)
+            src = h[g, c][:].rearrange("p t (b i) -> p b t i", i=4)
+            cut = on_vector // 4
+            if cut > 0:
+                nc.vector.tensor_copy(dst[:, :cut], src[:, :cut])
+            if cut < CHUNK // 4:
+                nc.scalar.copy(dst[:, cut:], src[:, cut:])
+
+        h_plane = held([P, GROUPS, S], U8, "h_plane")
+        h_codes = {}
+
+        def quantize_h(g, c):
+            cols = slice(CHUNK * c, CHUNK * (c + 1))
+            h_codes[g, c] = held([P, CHUNK], U32, f"h_codes{g}{c}")
+            nc.vector.quantize_mx(h_codes[g, c][:].bitcast(E4M3), h_plane[:, g, cols], h_bf[g, c][:])
+            nc.sync.dma_start(
+                out_2[g].rearrange("p m t -> p (m t)").bitcast(I32)[:, cols], h_codes[g, c][:].bitcast(I32))
+
+        w4 = []
+
+        def load_w4():
+            w4.append(held([P, GROUPS, N], I32, "tab1"))
+            nc.sync.dma_start(w4[0][:], w4_words.rearrange("a p c i -> p a (c i)").bitcast(I32))
+
+        def sig_pass(acc, b, c, g):
+            m = slice(P * b, P * (b + 1))
+            nc.tensor.matmul_mx(
+                acc[:], w4[0][:, g, m].bitcast(E4M3), w4_plane[4 * g : P, m],
+                h_codes[g, c][:].bitcast(E4M3), h_plane[:, g, CHUNK * c : CHUNK * (c + 1)],
+                start=(g == 0), stop=(g == GROUPS - 1))
+
+        def misfit(acc, b, c):
+            cols = slice(CHUNK * c, CHUNK * (c + 1))
+            diff = ring.tile([P, CHUNK], F32, name="diff")
+            nc.vector.tensor_tensor(diff[:], template[b // 2][:, b % 2, cols], acc[:], ALU.subtract)
+            y = held([P, CHUNK], F32, f"y{b}{c}")
+            nc.scalar.activation(y[:], diff[:], ACT.Square)
+            nc.sync.dma_start(out_0[P * b : P * (b + 1), cols], y[:])
+
+        deal_w3_words(0)
+        deal_w3_words(1)
+        load_w1(0, 1, 0, SPAN // 2)
+        load_w1(0, 1, SPAN // 2, SPAN)
+        gather_planes()
+        gather(0, 0)
+        gather(0, 1)
+        deal_w3_plane(0)
+        gather(1, 0)
+        skips = [bank() for t in range(PACK)]
+        for a in range(PASSES):
+            for t in range(PACK):
+                skip_pass(skips[t], 0, 0, t, a)
+        round_w1(0, 0, 0, SPAN, nc.scalar.copy)
+        load_w1(1, 0, 0, SPAN)
+        quantize_w1(0, 0)
+        firsts = [bank() for t in range(PACK)]
+        for t in range(PACK):
+            first_pass(firsts[t], 0, 0, t, 0)
+        round_w1(0, 1, 0, SPAN // 2, nc.scalar.copy)
+        round_w1(0, 1, SPAN // 2, SPAN, nc.scalar.copy)
+        load_w1(1, 1, 0, SPAN)
+        quantize_w1(0, 1)
+        gather(1, 1)
+        load_w4()
+        deal_w3_plane(1)
+        for t in range(PACK):
+            first_pass(firsts[t], 0, 0, t, 1)
+            combine(0, 0, t, firsts[t], skips[t])
+
+        round_w1(1, 0, 0, SPAN, nc.scalar.copy)
+        load_template(0)
+        slice_of_h(0, 1, 0)
+        round_w1(1, 1, 0, SPAN, nc.vector.tensor_copy)
+        load_template(1)
+        slice_of_h(0, 1, 1)
+        quantize_w1(1, 0)
+        slice_of_h(0, 1, 2)
+        quantize_w1(1, 1)
+        slice_of_h(0, 1, 3)
+
+        slice_of_h(1, 0, 0)
+        round_h(0, 0, 0)
+        slice_of_h(1, 0, 1)
+        round_h(0, 1, 512)
+        slice_of_h(1, 0, 2)
+        quantize_h(0, 0)
+        slice_of_h(1, 0, 3)
+        quantize_h(0, 1)
+
+        slice_of_h(1, 1, 0)
+        round_h(1, 0, 0)
+        slice_of_h(1, 1, 1)
+        quantize_h(1, 0)
+        slice_of_h(1, 1, 2)
+        slice_of_h(1, 1, 3)
+        sigs = []
+        for b in range(N // P):
+            acc = bank()
+            for g in range(GROUPS):
+                sig_pass(acc, b, 0, g)
+            sigs.append(acc)
+        round_h(1, 1, 256)
+        misfit(sigs[0], 0, 0)
+        quantize_h(1, 1)
+        misfit(sigs[1], 1, 0)
+        misfit(sigs[2], 2, 0)
+        misfit(sigs[3], 3, 0)
+        sigs = [bank() for b in range(N // P)]
+        for b in range(N // P):
+            sig_pass(sigs[b], b, 1, 0)
+        for b in range(N // P):
+            sig_pass(sigs[b], b, 1, 1)
+            misfit(sigs[b], b, 1)
+        for q in range(QUADS):
+            nc.sync.dma_start(
+                out_3[:, 4 * q : 4 * q + 4, :].rearrange("g r m -> r g m").bitcast(I32),
+                h_plane[32 * q : 32 * q + 4].bitcast(I32))

@@ -40,78 +40,82 @@ def tile_list_sonar_template_misfit_kernel(
         def held(shape, dtype, name):
             return keep.tile(shape, dtype, name=name, align_bytes=64)
 
+        def staged(shape, dtype, slot):
+            return stage.tile(shape, dtype, name=f"staged{slot}", align_bytes=64)
+
         offsets = keep.tile([P, S // 16], U16, name="offsets")
         nc.sync.dma_start(offsets[:], offs)
 
+        tab_rows = held([P, T // 4], I32, "tab_rows")
         tab_plane = held([P, T], U8, "tab_plane")
         w3_plane_raw = held([P, PASSES, H], U8, "w3_plane_raw")
         v_plane1 = held([P, S], U8, "v_plane1")
-        w4_plane = held([P, N], U8, "w4_plane")
         warm = held([P, 1], F32, "warm")
         warm_out = held([P, 1], F32, "warm_out")
+        nc.vector.memset(w3_plane_raw[:].rearrange("p a n -> p (a n)").bitcast(I32), 0)
         nc.vector.memset(tab_plane[:].bitcast(I32), 0)
         nc.vector.memset(warm[:], 0.0)
         nc.vector.memset(v_plane1[:].bitcast(I32), 0)
-        nc.gpsimd.memset(w3_plane_raw[:].rearrange("p a n -> p (a n)").bitcast(I32), 0)
         for q in range(QUADS):
-            nc.scalar.dma_start(
-                tab_plane[32 * q : 32 * q + 8, :].bitcast(I32),
+            nc.sync.dma_start(
+                tab_rows[32 * q : 32 * q + 8, :],
                 tab_scales[:, 4 * q : 4 * q + 4, :].bitcast(I32))
+        for q in range(QUADS):
+            nc.vector.tensor_copy(tab_plane[32 * q : 32 * q + 8, :].bitcast(I32), tab_rows[32 * q : 32 * q + 8, :])
         nc.scalar.activation(warm_out[:], warm[:], ACT.Tanh)
         for q in range(QUADS):
-            nc.gpsimd.dma_start(
+            nc.sync.dma_start(
                 w3_plane_raw[32 * q : 32 * q + 4].bitcast(I32),
                 w3_scales[:, 4 * q : 4 * q + 4, :].rearrange("a r n -> r a n").bitcast(I32))
         gain = held([P, GROUPS, PACK], F32, "gain")
-        nc.gpsimd.dma_start(gain[:], w2.rearrange("(g p t) -> p g t", p=P, t=PACK))
-        nc.gpsimd.memset(w4_plane[:].bitcast(I32), 0)
-        for q in range(QUADS):
-            nc.gpsimd.dma_start(
-                w4_plane[32 * q : 32 * q + 8, :].bitcast(I32),
-                w4_scales[:, 4 * q : 4 * q + 4, :].bitcast(I32))
 
         tab = {}
 
-        def load_tab(a):
-            tab[a] = held([P, T], I32, f"tab{a}")
+        def load_tab(a, slot):
+            tab[a] = staged([P, T], I32, slot)
             nc.sync.dma_start(tab[a][:], tab_words[a].rearrange("p t i -> p (t i)").bitcast(I32))
 
-        w3_raw = stage.tile([P, PASSES, 2 * H // 4], I32, name="staged1")
+        w3_raw = {}
+
+        def load_w3(g, name):
+            w3_raw[g] = held([P, PASSES, 2 * SPAN // 4], I32, name)
+            nc.sync.dma_start(
+                w3_raw[g][:],
+                w3_words[:, :, 2 * SPAN * g : 2 * SPAN * (g + 1)].rearrange("a p n -> p a n").bitcast(I32))
+
+        def load_gain():
+            nc.sync.dma_start(gain[:], w2.rearrange("(g p t) -> p g t", p=P, t=PACK))
 
         w1_raw = {}
 
-        def load_w1(g, a, lo, hi):
+        def load_w1(g, a, lo, hi, slot):
             if lo == 0:
-                w1_raw[g, a] = stage.tile([P, PACK, SPAN], F32, name=f"staged{a}")
+                w1_raw[g, a] = staged([P, PACK, SPAN], F32, slot)
             rows = w1[SPAN * a : SPAN * (a + 1), SPAN * g + lo : SPAN * g + hi]
             nc.sync.dma_start(w1_raw[g, a][:, :, lo:hi], rows.rearrange("(p i) c -> p i c", i=PACK))
 
         template = []
 
-        def load_template(u):
-            rows = stage.tile([P, 2, S], F32, name=f"staged{u}")
+        def load_template(u, slot):
+            rows = staged([P, 2, S], F32, slot)
             nc.sync.dma_start(rows[:], tpl[2 * P * u : 2 * P * (u + 1), :].rearrange("(b p) j -> p b j", p=P))
             template.append(rows)
 
-        nc.sync.dma_start(w3_raw[:], w3_words.rearrange("a p n -> p a n").bitcast(I32))
-        load_tab(0)
-        load_w1(0, 0, 0, SPAN)
-        load_tab(1)
 
         v_plane0 = held([P, S], U8, "v_plane0")
 
         def gather_planes():
             nc.vector.tensor_copy(v_plane0[:], tab_plane[:].indirect(offsets[:]))
             for q in range(QUADS):
-                nc.sync.dma_start(
+                nc.scalar.dma_start(
                     v_plane1[32 * q : 32 * q + 4, :].bitcast(I32),
                     v_plane0[32 * q + 4 : 32 * q + 8, :].bitcast(I32))
 
         v_plane = [v_plane0, v_plane1]
         v = {}
 
-        def gather(a, c):
-            v[a, c] = held([P, CHUNK], U32, f"v{a}{c}")
+        def gather(a, c, name=None):
+            v[a, c] = held([P, CHUNK], U32, name or f"v{a}{c}")
             cols = CHUNK // 16
             nc.vector.tensor_copy(v[a, c][:], tab[a][:].bitcast(U32).indirect(offsets[:, cols * c : cols * (c + 1)]))
 
@@ -122,10 +126,10 @@ def tile_list_sonar_template_misfit_kernel(
             w3[g] = held([P, PASSES, 2 * SPAN], U8, f"w3_{g}")
             nc.vector.tensor_copy(
                 w3[g][:].bitcast(U16).rearrange("p a (t m) -> p a t m", t=PACK),
-                w3_raw[:].bitcast(U16)[:, :, SPAN * g : SPAN * (g + 1)].rearrange("p a (m t) -> p a t m", t=PACK))
+                w3_raw[g][:].bitcast(U16).rearrange("p a (m t) -> p a t m", t=PACK))
 
-        def deal_w3_plane(g):
-            w3_plane[g] = held([P, PASSES, SPAN], U8, f"w3_plane{g}")
+        def deal_w3_plane(g, name=None):
+            w3_plane[g] = held([P, PASSES, SPAN], U8, name or f"w3_plane{g}")
             nc.vector.tensor_copy(
                 w3_plane[g][:].rearrange("p a (t m) -> p a t m", t=PACK),
                 w3_plane_raw[:, :, SPAN * g : SPAN * (g + 1)].rearrange("p a (m t) -> p a t m", t=PACK))
@@ -185,15 +189,12 @@ def tile_list_sonar_template_misfit_kernel(
 
         h_bf = {}
 
-        def round_h(g, c, on_vector):
-            h_bf[g, c] = held([P, CHUNK * PACK], BF16, f"h_bf{g}{c}")
+        def round_h(g, c, lo, hi, copy):
+            if lo == 0:
+                h_bf[g, c] = held([P, CHUNK * PACK], BF16, f"h_bf{g}{c}")
             dst = h_bf[g, c][:].rearrange("p (b i t) -> p b t i", i=4, t=PACK)
             src = h[g, c][:].rearrange("p t (b i) -> p b t i", i=4)
-            cut = on_vector // 4
-            if cut > 0:
-                nc.vector.tensor_copy(dst[:, :cut], src[:, :cut])
-            if cut < CHUNK // 4:
-                nc.scalar.copy(dst[:, cut:], src[:, cut:])
+            copy(dst[:, lo // 4 : hi // 4], src[:, lo // 4 : hi // 4])
 
         h_plane = held([P, GROUPS, S], U8, "h_plane")
         h_codes = {}
@@ -206,15 +207,24 @@ def tile_list_sonar_template_misfit_kernel(
                 out_2[g].rearrange("p m t -> p (m t)").bitcast(I32)[:, cols], h_codes[g, c][:].bitcast(I32))
 
         w4 = []
+        w4_plane = []
 
-        def load_w4():
-            w4.append(held([P, GROUPS, N], I32, "tab1"))
+        def load_w4(slot):
+            w4.append(staged([P, GROUPS, N], I32, slot))
             nc.sync.dma_start(w4[0][:], w4_words.rearrange("a p c i -> p a (c i)").bitcast(I32))
+
+        def load_w4_plane(name):
+            w4_plane.append(held([P, N], U8, name))
+            nc.gpsimd.memset(w4_plane[0][:].bitcast(I32), 0)
+            for q in range(QUADS):
+                nc.sync.dma_start(
+                    w4_plane[0][32 * q : 32 * q + 8, :].bitcast(I32),
+                    w4_scales[:, 4 * q : 4 * q + 4, :].bitcast(I32))
 
         def sig_pass(acc, b, c, g):
             m = slice(P * b, P * (b + 1))
             nc.tensor.matmul_mx(
-                acc[:], w4[0][:, g, m].bitcast(E4M3), w4_plane[4 * g : P, m],
+                acc[:], w4[0][:, g, m].bitcast(E4M3), w4_plane[0][4 * g : P, m],
                 h_codes[g, c][:].bitcast(E4M3), h_plane[:, g, CHUNK * c : CHUNK * (c + 1)],
                 start=(g == 0), stop=(g == GROUPS - 1))
 
@@ -226,73 +236,82 @@ def tile_list_sonar_template_misfit_kernel(
             nc.scalar.activation(y[:], diff[:], ACT.Square)
             nc.sync.dma_start(out_0[P * b : P * (b + 1), cols], y[:])
 
-        deal_w3_words(0)
-        deal_w3_words(1)
-        load_w1(0, 1, 0, SPAN // 2)
-        load_w1(0, 1, SPAN // 2, SPAN)
+        on_v, on_s = nc.vector.tensor_copy, nc.scalar.copy
+        load_w1(0, 0, 0, SPAN, 0)
+        load_gain()
+        load_w3(0, "w3_raw0")
+        load_tab(0, 3)
+        load_w1(0, 1, 0, SPAN, 1)
+        load_tab(1, 2)
         gather_planes()
+        deal_w3_words(0)
         gather(0, 0)
-        gather(0, 1)
-        deal_w3_plane(0)
-        gather(1, 0)
-        skips = [bank() for t in range(PACK)]
-        for a in range(PASSES):
-            for t in range(PACK):
-                skip_pass(skips[t], 0, 0, t, a)
-        round_w1(0, 0, 0, SPAN, nc.scalar.copy)
-        load_w1(1, 0, 0, SPAN)
+        round_w1(0, 0, 0, SPAN, on_s)
         quantize_w1(0, 0)
+        deal_w3_plane(0)
+        gather(0, 1)
+        load_w3(1, "tab_plane")
+        load_w1(1, 0, 0, SPAN, 0)
+        load_w1(1, 1, 0, SPAN, 3)
+        skips = [bank() for t in range(PACK)]
         firsts = [bank() for t in range(PACK)]
         for t in range(PACK):
             first_pass(firsts[t], 0, 0, t, 0)
-        round_w1(0, 1, 0, SPAN // 2, nc.scalar.copy)
-        round_w1(0, 1, SPAN // 2, SPAN, nc.scalar.copy)
-        load_w1(1, 1, 0, SPAN)
+            skip_pass(skips[t], 0, 0, t, 0)
+        round_w1(0, 1, 0, SPAN, on_s)
         quantize_w1(0, 1)
-        gather(1, 1)
-        load_w4()
-        deal_w3_plane(1)
+        gather(1, 0)
         for t in range(PACK):
             first_pass(firsts[t], 0, 0, t, 1)
+            skip_pass(skips[t], 0, 0, t, 1)
             combine(0, 0, t, firsts[t], skips[t])
-
-        round_w1(1, 0, 0, SPAN, nc.scalar.copy)
-        load_template(0)
-        slice_of_h(0, 1, 0)
-        round_w1(1, 1, 0, SPAN, nc.vector.tensor_copy)
-        load_template(1)
-        slice_of_h(0, 1, 1)
+            if t == 0:
+                gather(1, 1)
+            round_w1(1, 0, P * t, P * (t + 1), on_s)
         quantize_w1(1, 0)
-        slice_of_h(0, 1, 2)
+        load_w4(1)
+        load_template(0, 2)
+        load_w4_plane("w1_bf00")
+        load_template(1, 0)
+        round_w1(1, 1, 0, 256, on_v)
+        round_w1(1, 1, 256, 512, on_v)
         quantize_w1(1, 1)
-        slice_of_h(0, 1, 3)
+        deal_w3_words(1)
+        deal_w3_plane(1)
 
-        slice_of_h(1, 0, 0)
-        round_h(0, 0, 0)
-        slice_of_h(1, 0, 1)
-        round_h(0, 1, 512)
-        slice_of_h(1, 0, 2)
+        E = {"v": on_v, "s": on_s}
+
+        def round_part(g, c, part, who):
+            round_h(g, c, P * part, P * (part + 1), E[who[part]])
+
+        for t in range(PACK):
+            slice_of_h(0, 1, t)
+            round_part(0, 0, t, "vvss")
         quantize_h(0, 0)
-        slice_of_h(1, 0, 3)
+        for t in range(PACK):
+            slice_of_h(1, 0, t)
+            round_part(0, 1, t, "vvss")
         quantize_h(0, 1)
-
         slice_of_h(1, 1, 0)
-        round_h(1, 0, 0)
+        for t in range(PACK):
+            round_part(1, 0, t, "vvss")
         slice_of_h(1, 1, 1)
         quantize_h(1, 0)
         slice_of_h(1, 1, 2)
-        slice_of_h(1, 1, 3)
         sigs = []
         for b in range(N // P):
             acc = bank()
             for g in range(GROUPS):
                 sig_pass(acc, b, 0, g)
             sigs.append(acc)
-        round_h(1, 1, 256)
+            if b == 1:
+                slice_of_h(1, 1, 3)
         misfit(sigs[0], 0, 0)
-        quantize_h(1, 1)
         misfit(sigs[1], 1, 0)
+        for t in range(PACK):
+            round_part(1, 1, t, "vvss")
         misfit(sigs[2], 2, 0)
+        quantize_h(1, 1)
         misfit(sigs[3], 3, 0)
         sigs = [bank() for b in range(N // P)]
         for b in range(N // P):

@@ -50,11 +50,8 @@ def tile_list_sonar_template_misfit_kernel(
         tab_plane = held([P, T], U8, "tab_plane")
         w3_plane_raw = held([P, PASSES, H], U8, "w3_plane_raw")
         v_plane1 = held([P, S], U8, "v_plane1")
-        warm = held([P, 1], F32, "warm")
-        warm_out = held([P, 1], F32, "warm_out")
         nc.vector.memset(w3_plane_raw[:].rearrange("p a n -> p (a n)").bitcast(I32), 0)
         nc.vector.memset(tab_plane[:].bitcast(I32), 0)
-        nc.vector.memset(warm[:], 0.0)
         nc.vector.memset(v_plane1[:].bitcast(I32), 0)
         for q in range(QUADS):
             nc.sync.dma_start(
@@ -62,11 +59,10 @@ def tile_list_sonar_template_misfit_kernel(
                 tab_scales[:, 4 * q : 4 * q + 4, :].bitcast(I32))
         for q in range(QUADS):
             nc.vector.tensor_copy(tab_plane[32 * q : 32 * q + 8, :].bitcast(I32), tab_rows[32 * q : 32 * q + 8, :])
-        nc.scalar.activation(warm_out[:], warm[:], ACT.Tanh)
         for q in range(QUADS):
             nc.sync.dma_start(
-                w3_plane_raw[32 * q : 32 * q + 4].bitcast(I32),
-                w3_scales[:, 4 * q : 4 * q + 4, :].rearrange("a r n -> r a n").bitcast(I32))
+                w3_plane_raw[q:P:32].bitcast(I32),
+                w3_scales[:, q::4, :].rearrange("a r n -> r a n").bitcast(I32))
         gain = held([P, GROUPS, PACK], F32, "gain")
 
         tab = {}
@@ -108,8 +104,8 @@ def tile_list_sonar_template_misfit_kernel(
             nc.vector.tensor_copy(v_plane0[:], tab_plane[:].indirect(offsets[:]))
             for q in range(QUADS):
                 nc.scalar.dma_start(
-                    v_plane1[32 * q : 32 * q + 4, :].bitcast(I32),
-                    v_plane0[32 * q + 4 : 32 * q + 8, :].bitcast(I32))
+                    v_plane1[q:P:32, :].bitcast(I32),
+                    v_plane0[q + 4 : P : 32, :].bitcast(I32))
 
         v_plane = [v_plane0, v_plane1]
         v = {}
@@ -214,17 +210,17 @@ def tile_list_sonar_template_misfit_kernel(
             nc.sync.dma_start(w4[0][:], w4_words.rearrange("a p c i -> p a (c i)").bitcast(I32))
 
         def load_w4_plane(name):
-            w4_plane.append(held([P, N], U8, name))
-            nc.gpsimd.memset(w4_plane[0][:].bitcast(I32), 0)
+            w4_plane.append(held([P, GROUPS, N], U8, name))
+            nc.gpsimd.memset(w4_plane[0][:].rearrange("p a n -> p (a n)").bitcast(I32), 0)
             for q in range(QUADS):
                 nc.sync.dma_start(
-                    w4_plane[0][32 * q : 32 * q + 8, :].bitcast(I32),
-                    w4_scales[:, 4 * q : 4 * q + 4, :].bitcast(I32))
+                    w4_plane[0][q:P:32].bitcast(I32),
+                    w4_scales[:, q::4, :].rearrange("a r n -> r a n").bitcast(I32))
 
         def sig_pass(acc, b, c, g):
             m = slice(P * b, P * (b + 1))
             nc.tensor.matmul_mx(
-                acc[:], w4[0][:, g, m].bitcast(E4M3), w4_plane[0][4 * g : P, m],
+                acc[:], w4[0][:, g, m].bitcast(E4M3), w4_plane[0][:, g, m],
                 h_codes[g, c][:].bitcast(E4M3), h_plane[:, g, CHUNK * c : CHUNK * (c + 1)],
                 start=(g == 0), stop=(g == GROUPS - 1))
 
@@ -321,5 +317,5 @@ def tile_list_sonar_template_misfit_kernel(
             misfit(sigs[b], b, 1)
         for q in range(QUADS):
             nc.sync.dma_start(
-                out_3[:, 4 * q : 4 * q + 4, :].rearrange("g r m -> r g m").bitcast(I32),
-                h_plane[32 * q : 32 * q + 4].bitcast(I32))
+                out_3[:, q::4, :].rearrange("g r m -> r g m").bitcast(I32),
+                h_plane[q:P:32].bitcast(I32))

@@ -24,6 +24,7 @@ GROUPS = H // SPAN
 CHUNK = 512
 CHUNKS = S // CHUNK
 QUADS = 4
+ROWS = 16
 
 
 def tile_list_sonar_template_misfit_kernel(
@@ -34,113 +35,95 @@ def tile_list_sonar_template_misfit_kernel(
     with ExitStack() as ctx:
         keep = ctx.enter_context(tc.tile_pool(name="keep", bufs=1))
         ring = ctx.enter_context(tc.tile_pool(name="ring", bufs=3))
-        stage = ctx.enter_context(tc.tile_pool(name="stage", bufs=1))
         psum = ctx.enter_context(tc.psum_pool(name="psum", bufs=8))
 
         def held(shape, dtype, name):
             return keep.tile(shape, dtype, name=name, align_bytes=64)
 
-        def staged(shape, dtype, slot):
-            return stage.tile(shape, dtype, name=f"staged{slot}", align_bytes=64)
-
         offsets = keep.tile([P, S // 16], U16, name="offsets")
-        nc.sync.dma_start(offsets[:], offs)
-
-        tab_rows = held([P, T // 4], I32, "tab_rows")
-        tab_plane = held([P, T], U8, "tab_plane")
-        w3_plane_raw = held([P, PASSES, H], U8, "w3_plane_raw")
+        window = held([P, T], U8, "window")
+        weight_rows = held([P, PASSES, H], U8, "weight_rows")
+        v_plane0 = held([P, S], U8, "v_plane0")
         v_plane1 = held([P, S], U8, "v_plane1")
-        nc.vector.memset(w3_plane_raw[:].rearrange("p a n -> p (a n)").bitcast(I32), 0)
-        nc.vector.memset(tab_plane[:].bitcast(I32), 0)
-        nc.vector.memset(v_plane1[:].bitcast(I32), 0)
-        for q in range(QUADS):
-            nc.sync.dma_start(
-                tab_rows[32 * q : 32 * q + 8, :],
-                tab_scales[:, 4 * q : 4 * q + 4, :].bitcast(I32))
-        for q in range(QUADS):
-            nc.vector.tensor_copy(tab_plane[32 * q : 32 * q + 8, :].bitcast(I32), tab_rows[32 * q : 32 * q + 8, :])
-        for q in range(QUADS):
-            nc.sync.dma_start(
-                w3_plane_raw[q:P:32].bitcast(I32),
-                w3_scales[:, q::4, :].rearrange("a r n -> r a n").bitcast(I32))
+        v_plane = [v_plane0, v_plane1]
         gain = held([P, GROUPS, PACK], F32, "gain")
+        h_plane = held([P, GROUPS, S], U8, "h_plane")
+        tab, w1_raw, w1_bf, w1_codes, w1_plane, w3_raw, w3, w3_plane = {}, {}, {}, {}, {}, {}, {}, {}
+        v, h, h_bf, h_codes, template, w4, y = {}, {}, {}, {}, {}, {}, {}
 
-        tab = {}
-
-        def load_tab(a, slot):
-            tab[a] = staged([P, T], I32, slot)
+        def load_tab(a, name):
+            tab[a] = held([P, T], I32, name)
             nc.sync.dma_start(tab[a][:], tab_words[a].rearrange("p t i -> p (t i)").bitcast(I32))
 
-        w3_raw = {}
+        def load_tab_scales():
+            landed = held([P, T // 4], I32, "landed")
+            nc.sync.dma_start(landed[4 : 4 + ROWS, :], tab_scales[1].bitcast(I32))
+            for r in range(QUADS):
+                nc.sync.dma_start(landed[r:P:32, :], tab_scales[0, r::4, :].bitcast(I32))
+            for q in range(QUADS):
+                rows = slice(32 * q, 32 * q + 4 + (ROWS if q == 0 else 0))
+                nc.vector.tensor_copy(window[rows, :].bitcast(I32), landed[rows, :])
 
-        def load_w3(g, name):
-            w3_raw[g] = held([P, PASSES, 2 * SPAN // 4], I32, name)
-            nc.sync.dma_start(
-                w3_raw[g][:],
-                w3_words[:, :, 2 * SPAN * g : 2 * SPAN * (g + 1)].rearrange("a p n -> p a n").bitcast(I32))
+        def load_w3():
+            w3_raw[0] = held([P, PASSES, 2 * H // 4], I32, "w3_raw")
+            nc.sync.dma_start(w3_raw[0][:], w3_words.rearrange("a p n -> p a n").bitcast(I32))
+
+        def load_w3_scales():
+            for r in range(QUADS):
+                nc.sync.dma_start(
+                    weight_rows[r:P:32].bitcast(I32),
+                    w3_scales[:, r::4, :].rearrange("a q n -> q a n").bitcast(I32))
 
         def load_gain():
             nc.sync.dma_start(gain[:], w2.rearrange("(g p t) -> p g t", p=P, t=PACK))
 
-        w1_raw = {}
+        def load_w1(g, a, name):
+            w1_raw[g, a] = held([P, PACK, SPAN], F32, name)
+            rows = w1[SPAN * a : SPAN * (a + 1), SPAN * g : SPAN * (g + 1)]
+            nc.sync.dma_start(w1_raw[g, a][:], rows.rearrange("(p i) c -> p i c", i=PACK))
 
-        def load_w1(g, a, lo, hi, slot):
-            if lo == 0:
-                w1_raw[g, a] = staged([P, PACK, SPAN], F32, slot)
-            rows = w1[SPAN * a : SPAN * (a + 1), SPAN * g + lo : SPAN * g + hi]
-            nc.sync.dma_start(w1_raw[g, a][:, :, lo:hi], rows.rearrange("(p i) c -> p i c", i=PACK))
+        def load_template(u, name):
+            template[u] = held([P, 2, S], F32, name)
+            nc.sync.dma_start(template[u][:], tpl[2 * P * u : 2 * P * (u + 1), :].rearrange("(b p) j -> p b j", p=P))
 
-        template = []
+        def load_w4(name):
+            w4[0] = held([P, GROUPS, N], I32, name)
+            nc.sync.dma_start(w4[0][:], w4_words.rearrange("a p c i -> p a (c i)").bitcast(I32))
 
-        def load_template(u, slot):
-            rows = staged([P, 2, S], F32, slot)
-            nc.sync.dma_start(rows[:], tpl[2 * P * u : 2 * P * (u + 1), :].rearrange("(b p) j -> p b j", p=P))
-            template.append(rows)
-
-
-        v_plane0 = held([P, S], U8, "v_plane0")
+        def load_w4_scales():
+            for r in range(QUADS):
+                nc.sync.dma_start(
+                    weight_rows[r:P:32, :, 0:N].bitcast(I32),
+                    w4_scales[:, r::4, :].rearrange("a q n -> q a n").bitcast(I32))
 
         def gather_planes():
-            nc.vector.tensor_copy(v_plane0[:], tab_plane[:].indirect(offsets[:]))
-            for q in range(QUADS):
-                nc.scalar.dma_start(
-                    v_plane1[q:P:32, :].bitcast(I32),
-                    v_plane0[q + 4 : P : 32, :].bitcast(I32))
+            nc.vector.tensor_copy(v_plane0[:], window[:].indirect(offsets[:]))
+            for r in range(QUADS):
+                nc.sync.dma_start(v_plane1[r:P:32, :].bitcast(I32), v_plane0[4 + r : 4 + ROWS : 4, :].bitcast(I32))
 
-        v_plane = [v_plane0, v_plane1]
-        v = {}
-
-        def gather(a, c, name=None):
-            v[a, c] = held([P, CHUNK], U32, name or f"v{a}{c}")
+        def gather(a, c, name):
+            v[a, c] = held([P, CHUNK], U32, name)
             cols = CHUNK // 16
             nc.vector.tensor_copy(v[a, c][:], tab[a][:].bitcast(U32).indirect(offsets[:, cols * c : cols * (c + 1)]))
 
-        w3 = {}
-        w3_plane = {}
-
-        def deal_w3_words(g):
-            w3[g] = held([P, PASSES, 2 * SPAN], U8, f"w3_{g}")
-            nc.vector.tensor_copy(
+        def deal_w3_words(g, copy, name):
+            w3[g] = held([P, PASSES, 2 * SPAN], U8, name)
+            copy(
                 w3[g][:].bitcast(U16).rearrange("p a (t m) -> p a t m", t=PACK),
-                w3_raw[g][:].bitcast(U16).rearrange("p a (m t) -> p a t m", t=PACK))
+                w3_raw[0][:].bitcast(U16)[:, :, SPAN * g : SPAN * (g + 1)].rearrange("p a (m t) -> p a t m", t=PACK))
 
-        def deal_w3_plane(g, name=None):
-            w3_plane[g] = held([P, PASSES, SPAN], U8, name or f"w3_plane{g}")
+        def deal_w3_plane():
+            w3_plane[0] = held([P, PASSES, GROUPS, SPAN], U8, "w3_plane")
             nc.vector.tensor_copy(
-                w3_plane[g][:].rearrange("p a (t m) -> p a t m", t=PACK),
-                w3_plane_raw[:, :, SPAN * g : SPAN * (g + 1)].rearrange("p a (m t) -> p a t m", t=PACK))
+                w3_plane[0][:].rearrange("p a g (t m) -> p (a g) t m", t=PACK),
+                weight_rows[:].rearrange("p a (g m t) -> p (a g) t m", g=GROUPS, t=PACK))
 
-        w1_bf = {}
-
-        def round_w1(g, a, lo, hi, copy):
-            if lo == 0:
-                w1_bf[g, a] = held([P, SPAN * PACK], BF16, f"w1_bf{g}{a}")
+        def round_w1(g, a, lo, hi, copy, name=None):
+            if (g, a) not in w1_bf:
+                w1_bf[g, a] = held([P, SPAN * PACK], BF16, name)
             dealt = w1_bf[g, a][:].rearrange("p (t m i) -> p m i t", t=PACK, i=PACK)
             copy(dealt[:, lo // PACK : hi // PACK],
                  w1_raw[g, a][:, :, lo:hi].rearrange("p i (m t) -> p m i t", t=PACK))
-
-        w1_codes = {}
-        w1_plane = {}
 
         def quantize_w1(g, a):
             w1_codes[g, a] = held([P, SPAN], U32, f"w1_codes{g}{a}")
@@ -154,145 +137,165 @@ def tile_list_sonar_template_misfit_kernel(
             m = slice(P * t, P * (t + 1))
             nc.tensor.matmul_mx(
                 acc[:], w1_codes[g, a][:, m].bitcast(E4M3), w1_plane[g, a][:, m],
-                v[a, c][:].bitcast(E4M3), v_plane0[4 * a : P, CHUNK * c : CHUNK * (c + 1)],
+                v[a, c][:].bitcast(E4M3), v_plane[a][:, CHUNK * c : CHUNK * (c + 1)],
                 start=(a == 0), stop=(a == PASSES - 1))
 
         def skip_pass(acc, g, c, t, a):
             nc.tensor.matmul_mx(
-                acc[:], w3[g][:, a, 2 * P * t : 2 * P * (t + 1)].bitcast(E2M1), w3_plane[g][:, a, P * t : P * (t + 1)],
+                acc[:], w3[g][:, a, 2 * P * t : 2 * P * (t + 1)].bitcast(E2M1), w3_plane[0][:, a, g, P * t : P * (t + 1)],
                 v[a, c][:].bitcast(E4M3), v_plane[a][:, CHUNK * c : CHUNK * (c + 1)],
                 start=(a == 0), stop=(a == PASSES - 1))
 
-        h = {}
-
-        def combine(g, c, t, first, skip):
-            if t == 0:
-                h[g, c] = held([P, PACK, CHUNK], F32, f"h{g}{c}")
-            th = ring.tile([P, CHUNK], F32, name="th")
+        def combine(g, c, t, first, skip, name=None):
+            if g not in h:
+                h[g] = held([P, PACK, S], F32, f"h{g}")
+            if name is None:
+                th = ring.tile([P, CHUNK], F32, name="th")
+            else:
+                th = held([P, CHUNK], F32, name)
             nc.scalar.activation(th[:], first[:], ACT.Tanh)
-            nc.vector.scalar_tensor_tensor(h[g, c][:, t, :], th[:], gain[:, g, t : t + 1], skip[:], ALU.mult, ALU.add)
-            if t % 2 == 1:
-                rows = out_1[SPAN * g : SPAN * (g + 1), CHUNK * c : CHUNK * (c + 1)].rearrange("(p t) j -> p t j", t=PACK)
-                nc.sync.dma_start(rows[:, t - 1 : t + 1, :], h[g, c][:, t - 1 : t + 1, :])
+            nc.vector.scalar_tensor_tensor(
+                h[g][:, t, CHUNK * c : CHUNK * (c + 1)], th[:], gain[:, g, t : t + 1], skip[:], ALU.mult, ALU.add)
 
-        def slice_of_h(g, c, t):
+        def store_h(g, t0, t1, lo, hi):
+            rows = out_1[SPAN * g : SPAN * (g + 1), lo:hi].rearrange("(p t) j -> p t j", t=PACK)
+            nc.sync.dma_start(rows[:, t0:t1, :], h[g][:, t0:t1, lo:hi])
+
+        def slice_of_h(g, c, t, name=None):
             first, skip = bank(), bank()
             for a in range(PASSES):
                 first_pass(first, g, c, t, a)
             for a in range(PASSES):
                 skip_pass(skip, g, c, t, a)
-            combine(g, c, t, first, skip)
-
-        h_bf = {}
+            combine(g, c, t, first, skip, name)
 
         def round_h(g, c, lo, hi, copy):
-            if lo == 0:
+            if (g, c) not in h_bf:
                 h_bf[g, c] = held([P, CHUNK * PACK], BF16, f"h_bf{g}{c}")
             dst = h_bf[g, c][:].rearrange("p (b i t) -> p b t i", i=4, t=PACK)
-            src = h[g, c][:].rearrange("p t (b i) -> p b t i", i=4)
+            src = h[g][:, :, CHUNK * c : CHUNK * (c + 1)].rearrange("p t (b i) -> p b t i", i=4)
             copy(dst[:, lo // 4 : hi // 4], src[:, lo // 4 : hi // 4])
-
-        h_plane = held([P, GROUPS, S], U8, "h_plane")
-        h_codes = {}
 
         def quantize_h(g, c):
             cols = slice(CHUNK * c, CHUNK * (c + 1))
-            h_codes[g, c] = held([P, CHUNK], U32, f"h_codes{g}{c}")
-            nc.vector.quantize_mx(h_codes[g, c][:].bitcast(E4M3), h_plane[:, g, cols], h_bf[g, c][:])
+            if g not in h_codes:
+                h_codes[g] = held([P, S], U32, f"h_codes{g}")
+            nc.vector.quantize_mx(h_codes[g][:, cols].bitcast(E4M3), h_plane[:, g, cols], h_bf[g, c][:])
+
+        def store_codes(g, lo, hi):
             nc.sync.dma_start(
-                out_2[g].rearrange("p m t -> p (m t)").bitcast(I32)[:, cols], h_codes[g, c][:].bitcast(I32))
+                out_2[g].rearrange("p m t -> p (m t)").bitcast(I32)[:, lo:hi], h_codes[g][:, lo:hi].bitcast(I32))
 
-        w4 = []
-        w4_plane = []
-
-        def load_w4(slot):
-            w4.append(staged([P, GROUPS, N], I32, slot))
-            nc.sync.dma_start(w4[0][:], w4_words.rearrange("a p c i -> p a (c i)").bitcast(I32))
-
-        def load_w4_plane(name):
-            w4_plane.append(held([P, GROUPS, N], U8, name))
-            nc.gpsimd.memset(w4_plane[0][:].rearrange("p a n -> p (a n)").bitcast(I32), 0)
-            for q in range(QUADS):
+        def store_planes():
+            for r in range(QUADS):
                 nc.sync.dma_start(
-                    w4_plane[0][q:P:32].bitcast(I32),
-                    w4_scales[:, q::4, :].rearrange("a r n -> r a n").bitcast(I32))
+                    out_3[:, r::4, :].rearrange("g q m -> q g m").bitcast(I32),
+                    h_plane[r:P:32].bitcast(I32))
 
         def sig_pass(acc, b, c, g):
             m = slice(P * b, P * (b + 1))
+            cols = slice(CHUNK * c, CHUNK * (c + 1))
             nc.tensor.matmul_mx(
-                acc[:], w4[0][:, g, m].bitcast(E4M3), w4_plane[0][:, g, m],
-                h_codes[g, c][:].bitcast(E4M3), h_plane[:, g, CHUNK * c : CHUNK * (c + 1)],
+                acc[:], w4[0][:, g, m].bitcast(E4M3), weight_rows[:, g, m],
+                h_codes[g][:, cols].bitcast(E4M3), h_plane[:, g, cols],
                 start=(g == 0), stop=(g == GROUPS - 1))
 
         def misfit(acc, b, c):
             cols = slice(CHUNK * c, CHUNK * (c + 1))
+            if c not in y:
+                y[c] = held([P, N // P, CHUNK], F32, f"y{c}")
             diff = ring.tile([P, CHUNK], F32, name="diff")
             nc.vector.tensor_tensor(diff[:], template[b // 2][:, b % 2, cols], acc[:], ALU.subtract)
-            y = held([P, CHUNK], F32, f"y{b}{c}")
-            nc.scalar.activation(y[:], diff[:], ACT.Square)
-            nc.sync.dma_start(out_0[P * b : P * (b + 1), cols], y[:])
+            nc.scalar.activation(y[c][:, b, :], diff[:], ACT.Square)
+
+        def store_y(b0, b1, c):
+            rows = out_0[:, CHUNK * c : CHUNK * (c + 1)].rearrange("(b p) j -> p b j", p=P)
+            nc.sync.dma_start(rows[:, b0:b1, :], y[c][:, b0:b1, :])
 
         on_v, on_s = nc.vector.tensor_copy, nc.scalar.copy
-        load_w1(0, 0, 0, SPAN, 0)
+
+        def on_act(out, in_):
+            nc.scalar.activation(out, in_, ACT.Copy)
+
+        engine = {"v": on_v, "s": on_s}
+
+        def round_part(g, c, part, who):
+            round_h(g, c, P * part, P * (part + 1), engine[who[part]])
+
+        nc.vector.memset(weight_rows[:].rearrange("p a n -> p (a n)").bitcast(I32), 0)
+        nc.vector.memset(window[:].bitcast(I32), 0)
+        nc.vector.memset(v_plane1[:].bitcast(I32), 0)
+        nc.sync.dma_start(offsets[:], offs)
+        load_tab_scales()
+        load_tab(0, "slot_a")
+        load_w3()
+        load_w1(0, 0, "slot_b")
+        load_w3_scales()
+        load_tab(1, "slot_c")
+        load_w1(0, 1, "slot_d")
         load_gain()
-        load_w3(0, "w3_raw0")
-        load_tab(0, 3)
-        load_w1(0, 1, 0, SPAN, 1)
-        load_tab(1, 2)
+
         gather_planes()
-        deal_w3_words(0)
-        gather(0, 0)
-        round_w1(0, 0, 0, SPAN, on_s)
-        quantize_w1(0, 0)
-        deal_w3_plane(0)
-        gather(0, 1)
-        load_w3(1, "tab_plane")
-        load_w1(1, 0, 0, SPAN, 0)
-        load_w1(1, 1, 0, SPAN, 3)
+        gather(0, 0, "v00")
+        gather(0, 1, "window")
+        load_w1(1, 0, "slot_a")
+        deal_w3_words(0, on_s, "w3_0")
+        deal_w3_plane()
+        round_w1(0, 0, 0, SPAN, on_act, "w1_bf0")
+        load_w1(1, 1, "slot_b")
+        deal_w3_words(1, on_s, "w3_1")
         skips = [bank() for t in range(PACK)]
         firsts = [bank() for t in range(PACK)]
         for t in range(PACK):
-            first_pass(firsts[t], 0, 0, t, 0)
             skip_pass(skips[t], 0, 0, t, 0)
-        round_w1(0, 1, 0, SPAN, on_s)
+        gather(1, 0, "v10")
+        quantize_w1(0, 0)
+        for t in range(PACK):
+            first_pass(firsts[t], 0, 0, t, 0)
+        for t in range(PACK):
+            skip_pass(skips[t], 0, 0, t, 1)
+        round_w1(0, 1, 0, 320, on_v, "w1_bf0")
+        round_w1(0, 1, 320, SPAN, on_s)
         quantize_w1(0, 1)
-        gather(1, 0)
+        load_w4("w3_raw")
+        gather(1, 1, "w1_bf0")
+        load_template(0, "slot_c")
+        load_template(1, "slot_d")
+        load_w4_scales()
         for t in range(PACK):
             first_pass(firsts[t], 0, 0, t, 1)
-            skip_pass(skips[t], 0, 0, t, 1)
+        combine(0, 0, 0, firsts[0], skips[0], "w1_bf10")
+        for t in range(1, PACK):
             combine(0, 0, t, firsts[t], skips[t])
-            if t == 0:
-                gather(1, 1)
-            round_w1(1, 0, P * t, P * (t + 1), on_s)
+            round_w1(1, 0, P * (t - 1), P * t, on_s, "w1_bf10")
+        slice_of_h(0, 1, 0, "w1_bf11")
+        round_w1(1, 0, 3 * P, SPAN, on_s)
         quantize_w1(1, 0)
-        load_w4(1)
-        load_template(0, 2)
-        load_w4_plane("w1_bf00")
-        load_template(1, 0)
-        round_w1(1, 1, 0, 256, on_v)
-        round_w1(1, 1, 256, 512, on_v)
+        slice_of_h(0, 1, 1)
+        store_h(0, 0, 2, 0, S)
+        round_w1(1, 1, 0, 256, on_v, "w1_bf11")
+        round_w1(1, 1, 256, 384, on_s)
+        slice_of_h(0, 1, 2)
+        round_w1(1, 1, 384, 512, on_s)
         quantize_w1(1, 1)
-        deal_w3_words(1)
-        deal_w3_plane(1)
-
-        E = {"v": on_v, "s": on_s}
-
-        def round_part(g, c, part, who):
-            round_h(g, c, P * part, P * (part + 1), E[who[part]])
-
-        for t in range(PACK):
-            slice_of_h(0, 1, t)
-            round_part(0, 0, t, "vvss")
-        quantize_h(0, 0)
+        slice_of_h(0, 1, 3)
+        store_h(0, 2, 4, 0, S)
         for t in range(PACK):
             slice_of_h(1, 0, t)
-            round_part(0, 1, t, "vvss")
+            if t % 2 == 1:
+                store_h(1, t - 1, t + 1, 0, CHUNK)
+            round_part(0, 0, t, "vvss")
+            round_part(0, 1, t, "ssvv")
+        quantize_h(0, 0)
         quantize_h(0, 1)
+        store_codes(0, 0, S)
         slice_of_h(1, 1, 0)
         for t in range(PACK):
             round_part(1, 0, t, "vvss")
         slice_of_h(1, 1, 1)
+        store_h(1, 0, 2, CHUNK, S)
         quantize_h(1, 0)
+        store_codes(1, 0, CHUNK)
         slice_of_h(1, 1, 2)
         sigs = []
         for b in range(N // P):
@@ -302,20 +305,22 @@ def tile_list_sonar_template_misfit_kernel(
             sigs.append(acc)
             if b == 1:
                 slice_of_h(1, 1, 3)
+                store_h(1, 2, 4, CHUNK, S)
         misfit(sigs[0], 0, 0)
         misfit(sigs[1], 1, 0)
+        store_y(0, 2, 0)
         for t in range(PACK):
             round_part(1, 1, t, "vvss")
         misfit(sigs[2], 2, 0)
         quantize_h(1, 1)
+        store_codes(1, CHUNK, S)
+        store_planes()
         misfit(sigs[3], 3, 0)
+        store_y(2, 4, 0)
         sigs = [bank() for b in range(N // P)]
         for b in range(N // P):
             sig_pass(sigs[b], b, 1, 0)
         for b in range(N // P):
             sig_pass(sigs[b], b, 1, 1)
             misfit(sigs[b], b, 1)
-        for q in range(QUADS):
-            nc.sync.dma_start(
-                out_3[:, q::4, :].rearrange("g r m -> r g m").bitcast(I32),
-                h_plane[q:P:32].bitcast(I32))
+            store_y(b, b + 1, 1)

@@ -25,6 +25,8 @@ CHUNK = 512
 CHUNKS = S // CHUNK
 QUADS = 4
 ROWS = 16
+H_ROW = 4
+W4_ROW = 8
 
 
 def tile_list_sonar_template_misfit_kernel(
@@ -36,70 +38,67 @@ def tile_list_sonar_template_misfit_kernel(
         keep = ctx.enter_context(tc.tile_pool(name="keep", bufs=1))
         ring = ctx.enter_context(tc.tile_pool(name="ring", bufs=3))
         psum = ctx.enter_context(tc.psum_pool(name="psum", bufs=8))
+        stage = ctx.enter_context(tc.tile_pool(name="stage", bufs=1))
+
+        def staged(shape, dtype, name, kib):
+            return stage.tile(shape, dtype, name=name, align_bytes=64, offset=1024 * kib)
 
         def held(shape, dtype, name):
             return keep.tile(shape, dtype, name=name, align_bytes=64)
 
         offsets = keep.tile([P, S // 16], U16, name="offsets")
-        window = held([P, T], U8, "window")
-        weight_rows = held([P, PASSES, H], U8, "weight_rows")
-        v_plane0 = held([P, S], U8, "v_plane0")
-        v_plane1 = held([P, S], U8, "v_plane1")
-        v_plane = [v_plane0, v_plane1]
+        window = staged([P, T], U8, "window", 23)
+        w3_rows = held([P, PASSES, H], U8, "w3_rows")
+        picked = held([P, S], U8, "picked")
+        v_plane = held([P, PASSES, S], U8, "v_plane")
+        w3_plane = held([P, PASSES, H], U8, "w3_plane")
         gain = held([P, GROUPS, PACK], F32, "gain")
         h_plane = held([P, GROUPS, S], U8, "h_plane")
-        tab, w1_raw, w1_bf, w1_codes, w1_plane, w3_raw, w3, w3_plane = {}, {}, {}, {}, {}, {}, {}, {}
+        tab, w1_raw, w1_bf, w1_codes, w1_plane, w3_raw, w3, w4_plane = {}, {}, {}, {}, {}, {}, {}, {}
         v, h, h_bf, h_codes, template, w4, y = {}, {}, {}, {}, {}, {}, {}
 
-        def load_tab(a, name):
-            tab[a] = held([P, T], I32, name)
+        def load_tab(a, kib):
+            tab[a] = staged([P, T], I32, f"tab{a}", kib)
             nc.sync.dma_start(tab[a][:], tab_words[a].rearrange("p t i -> p (t i)").bitcast(I32))
 
-        def load_tab_scales():
-            landed = held([P, T // 4], I32, "landed")
-            nc.sync.dma_start(landed[4 : 4 + ROWS, :], tab_scales[1].bitcast(I32))
-            for r in range(QUADS):
-                nc.sync.dma_start(landed[r:P:32, :], tab_scales[0, r::4, :].bitcast(I32))
+        def load_rows(tile, scales):
+            nc.sync.dma_start(tile[0 : PASSES * ROWS, :].bitcast(I32), scales.rearrange("a u n -> u a n").bitcast(I32))
+
+        def spread(plane, rows):
             for q in range(QUADS):
-                rows = slice(32 * q, 32 * q + 4 + (ROWS if q == 0 else 0))
-                nc.vector.tensor_copy(window[rows, :].bitcast(I32), landed[rows, :])
+                nc.sync.dma_start(plane[32 * q : 32 * q + 4].bitcast(I32), rows[8 * q : 8 * q + 8, :].bitcast(I32))
 
         def load_w3():
             w3_raw[0] = held([P, PASSES, 2 * H // 4], I32, "w3_raw")
             nc.sync.dma_start(w3_raw[0][:], w3_words.rearrange("a p n -> p a n").bitcast(I32))
 
-        def load_w3_scales():
-            for r in range(QUADS):
-                nc.sync.dma_start(
-                    weight_rows[r:P:32].bitcast(I32),
-                    w3_scales[:, r::4, :].rearrange("a q n -> q a n").bitcast(I32))
-
         def load_gain():
             nc.sync.dma_start(gain[:], w2.rearrange("(g p t) -> p g t", p=P, t=PACK))
 
-        def load_w1(g, a, name):
-            w1_raw[g, a] = held([P, PACK, SPAN], F32, name)
+        def load_w1(g, a, kib):
+            w1_raw[g, a] = staged([P, PACK, SPAN], F32, f"w1_raw{g}{a}", kib)
             rows = w1[SPAN * a : SPAN * (a + 1), SPAN * g : SPAN * (g + 1)]
             nc.sync.dma_start(w1_raw[g, a][:], rows.rearrange("(p i) c -> p i c", i=PACK))
 
-        def load_template(u, name):
-            template[u] = held([P, 2, S], F32, name)
+        def load_template(u, kib):
+            template[u] = staged([P, 2, S], F32, f"template{u}", kib)
             nc.sync.dma_start(template[u][:], tpl[2 * P * u : 2 * P * (u + 1), :].rearrange("(b p) j -> p b j", p=P))
 
-        def load_w4(name):
-            w4[0] = held([P, GROUPS, N], I32, name)
+        def load_w4(kib):
+            w4[0] = staged([P, GROUPS, N], I32, "w4", kib)
             nc.sync.dma_start(w4[0][:], w4_words.rearrange("a p c i -> p a (c i)").bitcast(I32))
 
-        def load_w4_scales():
+        def load_w4_scales(kib):
+            w4_plane[0] = staged([P, GROUPS, N], U8, "w4_plane", kib)
+            nc.vector.memset(w4_plane[0][:].rearrange("p a n -> p (a n)").bitcast(I32), 0)
             for r in range(QUADS):
                 nc.sync.dma_start(
-                    weight_rows[r:P:32, :, 0:N].bitcast(I32),
+                    w4_plane[0][W4_ROW + r : P : 32].bitcast(I32),
                     w4_scales[:, r::4, :].rearrange("a q n -> q a n").bitcast(I32))
 
         def gather_planes():
-            nc.vector.tensor_copy(v_plane0[:], window[:].indirect(offsets[:]))
-            for r in range(QUADS):
-                nc.sync.dma_start(v_plane1[r:P:32, :].bitcast(I32), v_plane0[4 + r : 4 + ROWS : 4, :].bitcast(I32))
+            nc.vector.tensor_copy(picked[:], window[:].indirect(offsets[:]))
+            spread(v_plane, picked)
 
         def gather(a, c, name):
             v[a, c] = held([P, CHUNK], U32, name)
@@ -112,11 +111,15 @@ def tile_list_sonar_template_misfit_kernel(
                 w3[g][:].bitcast(U16).rearrange("p a (t m) -> p a t m", t=PACK),
                 w3_raw[0][:].bitcast(U16)[:, :, SPAN * g : SPAN * (g + 1)].rearrange("p a (m t) -> p a t m", t=PACK))
 
+        def load_w3_scales():
+            for r in range(QUADS):
+                nc.sync.dma_start(
+                    w3_rows[r:P:32].bitcast(I32), w3_scales[:, r::4, :].rearrange("a q n -> q a n").bitcast(I32))
+
         def deal_w3_plane():
-            w3_plane[0] = held([P, PASSES, GROUPS, SPAN], U8, "w3_plane")
             nc.vector.tensor_copy(
-                w3_plane[0][:].rearrange("p a g (t m) -> p (a g) t m", t=PACK),
-                weight_rows[:].rearrange("p a (g m t) -> p (a g) t m", g=GROUPS, t=PACK))
+                w3_plane[:].rearrange("p a (g t m) -> p (a g) t m", g=GROUPS, t=PACK),
+                w3_rows[:].rearrange("p a (g m t) -> p (a g) t m", g=GROUPS, t=PACK))
 
         def round_w1(g, a, lo, hi, copy, name=None):
             if (g, a) not in w1_bf:
@@ -137,13 +140,13 @@ def tile_list_sonar_template_misfit_kernel(
             m = slice(P * t, P * (t + 1))
             nc.tensor.matmul_mx(
                 acc[:], w1_codes[g, a][:, m].bitcast(E4M3), w1_plane[g, a][:, m],
-                v[a, c][:].bitcast(E4M3), v_plane[a][:, CHUNK * c : CHUNK * (c + 1)],
+                v[a, c][:].bitcast(E4M3), v_plane[:, a, CHUNK * c : CHUNK * (c + 1)],
                 start=(a == 0), stop=(a == PASSES - 1))
 
         def skip_pass(acc, g, c, t, a):
             nc.tensor.matmul_mx(
-                acc[:], w3[g][:, a, 2 * P * t : 2 * P * (t + 1)].bitcast(E2M1), w3_plane[0][:, a, g, P * t : P * (t + 1)],
-                v[a, c][:].bitcast(E4M3), v_plane[a][:, CHUNK * c : CHUNK * (c + 1)],
+                acc[:], w3[g][:, a, 2 * P * t : 2 * P * (t + 1)].bitcast(E2M1), w3_plane[:, a, SPAN * g + P * t : SPAN * g + P * (t + 1)],
+                v[a, c][:].bitcast(E4M3), v_plane[:, a, CHUNK * c : CHUNK * (c + 1)],
                 start=(a == 0), stop=(a == PASSES - 1))
 
         def combine(g, c, t, first, skip, name=None):
@@ -180,7 +183,7 @@ def tile_list_sonar_template_misfit_kernel(
             cols = slice(CHUNK * c, CHUNK * (c + 1))
             if g not in h_codes:
                 h_codes[g] = held([P, S], U32, f"h_codes{g}")
-            nc.vector.quantize_mx(h_codes[g][:, cols].bitcast(E4M3), h_plane[:, g, cols], h_bf[g, c][:])
+            nc.vector.quantize_mx(h_codes[g][:, cols].bitcast(E4M3), h_plane[H_ROW:P, g, cols], h_bf[g, c][:])
 
         def store_codes(g, lo, hi):
             nc.sync.dma_start(
@@ -190,14 +193,14 @@ def tile_list_sonar_template_misfit_kernel(
             for r in range(QUADS):
                 nc.sync.dma_start(
                     out_3[:, r::4, :].rearrange("g q m -> q g m").bitcast(I32),
-                    h_plane[r:P:32].bitcast(I32))
+                    h_plane[H_ROW + r : P : 32].bitcast(I32))
 
         def sig_pass(acc, b, c, g):
             m = slice(P * b, P * (b + 1))
             cols = slice(CHUNK * c, CHUNK * (c + 1))
             nc.tensor.matmul_mx(
-                acc[:], w4[0][:, g, m].bitcast(E4M3), weight_rows[:, g, m],
-                h_codes[g][:, cols].bitcast(E4M3), h_plane[:, g, cols],
+                acc[:], w4[0][:, g, m].bitcast(E4M3), w4_plane[0][W4_ROW:P, g, m],
+                h_codes[g][:, cols].bitcast(E4M3), h_plane[H_ROW:P, g, cols],
                 start=(g == 0), stop=(g == GROUPS - 1))
 
         def misfit(acc, b, c):
@@ -222,48 +225,48 @@ def tile_list_sonar_template_misfit_kernel(
         def round_part(g, c, part, who):
             round_h(g, c, P * part, P * (part + 1), engine[who[part]])
 
-        nc.vector.memset(weight_rows[:].rearrange("p a n -> p (a n)").bitcast(I32), 0)
-        nc.vector.memset(window[:].bitcast(I32), 0)
-        nc.vector.memset(v_plane1[:].bitcast(I32), 0)
+        nc.vector.memset(w3_rows[:].rearrange("p a n -> p (a n)").bitcast(I32), 0)
+        nc.vector.memset(window[32:64, :].bitcast(I32), 0)
+        nc.vector.memset(window[64:P, :].bitcast(I32), 0)
+        nc.vector.memset(v_plane[:].rearrange("p a n -> p (a n)").bitcast(I32), 0)
+        load_rows(window, tab_scales)
         nc.sync.dma_start(offsets[:], offs)
-        load_tab_scales()
-        load_tab(0, "slot_a")
-        load_w3()
-        load_w1(0, 0, "slot_b")
-        load_w3_scales()
-        load_tab(1, "slot_c")
-        load_w1(0, 1, "slot_d")
         load_gain()
-
+        load_tab(0, 64)
+        load_w3_scales()
+        load_w3()
+        load_w1(0, 0, 48)
         gather_planes()
+        load_tab(1, 24)
+        load_w1(0, 1, 16)
         gather(0, 0, "v00")
-        gather(0, 1, "window")
-        load_w1(1, 0, "slot_a")
-        deal_w3_words(0, on_s, "w3_0")
         deal_w3_plane()
-        round_w1(0, 0, 0, SPAN, on_act, "w1_bf0")
-        load_w1(1, 1, "slot_b")
+        gather(0, 1, "v01")
+        deal_w3_words(0, on_s, "w3_0")
+        round_w1(0, 0, 0, SPAN, on_act, "w1_bf00")
         deal_w3_words(1, on_s, "w3_1")
         skips = [bank() for t in range(PACK)]
         firsts = [bank() for t in range(PACK)]
         for t in range(PACK):
             skip_pass(skips[t], 0, 0, t, 0)
-        gather(1, 0, "v10")
         quantize_w1(0, 0)
+        gather(1, 0, "v10")
         for t in range(PACK):
             first_pass(firsts[t], 0, 0, t, 0)
         for t in range(PACK):
             skip_pass(skips[t], 0, 0, t, 1)
-        round_w1(0, 1, 0, 320, on_v, "w1_bf0")
+        load_w1(1, 0, 60)
+        load_w1(1, 1, 68)
+        round_w1(0, 1, 0, 320, on_v, "w1_bf01")
         round_w1(0, 1, 320, SPAN, on_s)
         quantize_w1(0, 1)
-        load_w4("w3_raw")
-        gather(1, 1, "w1_bf0")
-        load_template(0, "slot_c")
-        load_template(1, "slot_d")
-        load_w4_scales()
+        gather(1, 1, "w1_bf01")
         for t in range(PACK):
             first_pass(firsts[t], 0, 0, t, 1)
+        load_w4(48)
+        load_w4_scales(52)
+        load_template(0, 12)
+        load_template(1, 20)
         combine(0, 0, 0, firsts[0], skips[0], "w1_bf10")
         for t in range(1, PACK):
             combine(0, 0, t, firsts[t], skips[t])

@@ -36,7 +36,7 @@ def tile_list_sonar_template_misfit_kernel(
     nc = tc.nc
     with ExitStack() as ctx:
         keep = ctx.enter_context(tc.tile_pool(name="keep", bufs=1))
-        ring = ctx.enter_context(tc.tile_pool(name="ring", bufs=3))
+        ring = ctx.enter_context(tc.tile_pool(name="ring", bufs=4))
         psum = ctx.enter_context(tc.psum_pool(name="psum", bufs=8))
         stage = ctx.enter_context(tc.tile_pool(name="stage", bufs=1))
 
@@ -55,7 +55,8 @@ def tile_list_sonar_template_misfit_kernel(
         gain = held([P, GROUPS, PACK], F32, "gain")
         h_plane = held([P, GROUPS, S], U8, "h_plane")
         tab, w1_raw, w1_bf, w1_codes, w1_plane, w3_raw, w3, w4_plane = {}, {}, {}, {}, {}, {}, {}, {}
-        v, h, h_bf, h_codes, template, w4, y = {}, {}, {}, {}, {}, {}, {}
+        v, h, h_bf, h_codes, template, w4 = {}, {}, {}, {}, {}, {}
+        y = held([P, N // P, S], F32, "y")
 
         def load_tab(a, kib):
             tab[a] = staged([P, T], I32, f"tab{a}", kib)
@@ -136,54 +137,60 @@ def tile_list_sonar_template_misfit_kernel(
         def bank():
             return psum.tile([P, CHUNK], F32, name="bank")
 
-        def first_pass(acc, g, c, t, a):
+        def picked_operand(a, lo, hi):
+            c, at = divmod(lo, CHUNK)
+            return v[a, c][:, at : at + hi - lo].bitcast(E4M3), v_plane[:, a, lo:hi]
+
+        def first_pass(acc, g, lo, hi, t, a):
             m = slice(P * t, P * (t + 1))
             nc.tensor.matmul_mx(
-                acc[:], w1_codes[g, a][:, m].bitcast(E4M3), w1_plane[g, a][:, m],
-                v[a, c][:].bitcast(E4M3), v_plane[:, a, CHUNK * c : CHUNK * (c + 1)],
+                acc, w1_codes[g, a][:, m].bitcast(E4M3), w1_plane[g, a][:, m], *picked_operand(a, lo, hi),
                 start=(a == 0), stop=(a == PASSES - 1))
 
-        def skip_pass(acc, g, c, t, a):
+        def skip_pass(acc, g, lo, hi, t, a):
+            at = SPAN * g + P * t
             nc.tensor.matmul_mx(
-                acc[:], w3[g][:, a, 2 * P * t : 2 * P * (t + 1)].bitcast(E2M1), w3_plane[:, a, SPAN * g + P * t : SPAN * g + P * (t + 1)],
-                v[a, c][:].bitcast(E4M3), v_plane[:, a, CHUNK * c : CHUNK * (c + 1)],
-                start=(a == 0), stop=(a == PASSES - 1))
+                acc, w3[g][:, a, 2 * P * t : 2 * P * (t + 1)].bitcast(E2M1), w3_plane[:, a, at : at + P],
+                *picked_operand(a, lo, hi), start=(a == 0), stop=(a == PASSES - 1))
 
-        def combine(g, c, t, first, skip, name=None):
+        def combine(g, lo, hi, t, first, skip, name=None):
             if g not in h:
                 h[g] = held([P, PACK, S], F32, f"h{g}")
             if name is None:
-                th = ring.tile([P, CHUNK], F32, name="th")
+                th = ring.tile([P, hi - lo], F32, name="th")
             else:
-                th = held([P, CHUNK], F32, name)
-            nc.scalar.activation(th[:], first[:], ACT.Tanh)
-            nc.vector.scalar_tensor_tensor(
-                h[g][:, t, CHUNK * c : CHUNK * (c + 1)], th[:], gain[:, g, t : t + 1], skip[:], ALU.mult, ALU.add)
+                th = held([P, hi - lo], F32, name)
+            nc.scalar.activation(th[:], first, ACT.Tanh)
+            nc.vector.scalar_tensor_tensor(h[g][:, t, lo:hi], th[:], gain[:, g, t : t + 1], skip, ALU.mult, ALU.add)
 
         def store_h(g, t0, t1, lo, hi):
             rows = out_1[SPAN * g : SPAN * (g + 1), lo:hi].rearrange("(p t) j -> p t j", t=PACK)
             nc.sync.dma_start(rows[:, t0:t1, :], h[g][:, t0:t1, lo:hi])
 
-        def slice_of_h(g, c, t, name=None):
-            first, skip = bank(), bank()
+        def slice_of_h(g, lo, hi, t):
+            if hi - lo == CHUNK:
+                first, skip = bank()[:], bank()[:]
+            else:
+                both = bank()
+                first, skip = both[:, 0 : hi - lo], both[:, hi - lo : 2 * (hi - lo)]
             for a in range(PASSES):
-                first_pass(first, g, c, t, a)
+                first_pass(first, g, lo, hi, t, a)
             for a in range(PASSES):
-                skip_pass(skip, g, c, t, a)
-            combine(g, c, t, first, skip, name)
+                skip_pass(skip, g, lo, hi, t, a)
+            combine(g, lo, hi, t, first, skip)
 
-        def round_h(g, c, lo, hi, copy):
-            if (g, c) not in h_bf:
-                h_bf[g, c] = held([P, CHUNK * PACK], BF16, f"h_bf{g}{c}")
-            dst = h_bf[g, c][:].rearrange("p (b i t) -> p b t i", i=4, t=PACK)
-            src = h[g][:, :, CHUNK * c : CHUNK * (c + 1)].rearrange("p t (b i) -> p b t i", i=4)
+        def round_h(g, lo, hi, copy):
+            if g not in h_bf:
+                h_bf[g] = held([P, S * PACK], BF16, f"h_bf{g}")
+            dst = h_bf[g][:].rearrange("p (b i t) -> p b t i", i=4, t=PACK)
+            src = h[g][:].rearrange("p t (b i) -> p b t i", i=4)
             copy(dst[:, lo // 4 : hi // 4], src[:, lo // 4 : hi // 4])
 
-        def quantize_h(g, c):
-            cols = slice(CHUNK * c, CHUNK * (c + 1))
+        def quantize_h(g, lo, hi):
             if g not in h_codes:
                 h_codes[g] = held([P, S], U32, f"h_codes{g}")
-            nc.vector.quantize_mx(h_codes[g][:, cols].bitcast(E4M3), h_plane[H_ROW:P, g, cols], h_bf[g, c][:])
+            nc.vector.quantize_mx(
+                h_codes[g][:, lo:hi].bitcast(E4M3), h_plane[H_ROW:P, g, lo:hi], h_bf[g][:, PACK * lo : PACK * hi])
 
         def store_codes(g, lo, hi):
             nc.sync.dma_start(
@@ -195,35 +202,28 @@ def tile_list_sonar_template_misfit_kernel(
                     out_3[:, r::4, :].rearrange("g q m -> q g m").bitcast(I32),
                     h_plane[H_ROW + r : P : 32].bitcast(I32))
 
-        def sig_pass(acc, b, c, g):
+        def sig_pass(acc, b, lo, hi, g, start, stop):
             m = slice(P * b, P * (b + 1))
-            cols = slice(CHUNK * c, CHUNK * (c + 1))
             nc.tensor.matmul_mx(
-                acc[:], w4[0][:, g, m].bitcast(E4M3), w4_plane[0][W4_ROW:P, g, m],
-                h_codes[g][:, cols].bitcast(E4M3), h_plane[H_ROW:P, g, cols],
-                start=(g == 0), stop=(g == GROUPS - 1))
+                acc, w4[0][:, g, m].bitcast(E4M3), w4_plane[0][W4_ROW:P, g, m],
+                h_codes[g][:, lo:hi].bitcast(E4M3), h_plane[H_ROW:P, g, lo:hi], start=start, stop=stop)
 
-        def misfit(acc, b, c):
-            cols = slice(CHUNK * c, CHUNK * (c + 1))
-            if c not in y:
-                y[c] = held([P, N // P, CHUNK], F32, f"y{c}")
-            diff = ring.tile([P, CHUNK], F32, name="diff")
-            nc.vector.tensor_tensor(diff[:], template[b // 2][:, b % 2, cols], acc[:], ALU.subtract)
-            nc.scalar.activation(y[c][:, b, :], diff[:], ACT.Square)
+        def misfit(acc, b0, b1, lo, hi):
+            n = b1 - b0
+            diff = ring.tile([P, n, hi - lo], F32, name="diff")
+            nc.vector.tensor_tensor(
+                diff[:], template[b0 // 2][:, b0 % 2 : b0 % 2 + n, lo:hi],
+                acc.rearrange("p (b j) -> p b j", b=n), ALU.subtract)
+            nc.scalar.activation(y[:, b0:b1, lo:hi], diff[:], ACT.Square)
 
-        def store_y(b0, b1, c):
-            rows = out_0[:, CHUNK * c : CHUNK * (c + 1)].rearrange("(b p) j -> p b j", p=P)
-            nc.sync.dma_start(rows[:, b0:b1, :], y[c][:, b0:b1, :])
+        def store_y(b0, b1, lo, hi):
+            rows = out_0[:, lo:hi].rearrange("(b p) j -> p b j", p=P)
+            nc.sync.dma_start(rows[:, b0:b1, :], y[:, b0:b1, lo:hi])
 
         on_v, on_s = nc.vector.tensor_copy, nc.scalar.copy
 
         def on_act(out, in_):
             nc.scalar.activation(out, in_, ACT.Copy)
-
-        engine = {"v": on_v, "s": on_s}
-
-        def round_part(g, c, part, who):
-            round_h(g, c, P * part, P * (part + 1), engine[who[part]])
 
         nc.vector.memset(w3_rows[:].rearrange("p a n -> p (a n)").bitcast(I32), 0)
         nc.vector.memset(window[32:64, :].bitcast(I32), 0)
@@ -245,85 +245,90 @@ def tile_list_sonar_template_misfit_kernel(
         deal_w3_words(0, on_s, "w3_0")
         round_w1(0, 0, 0, SPAN, on_act, "w1_bf00")
         deal_w3_words(1, on_s, "w3_1")
-        skips = [bank() for t in range(PACK)]
-        firsts = [bank() for t in range(PACK)]
+        skips = [bank()[:] for t in range(PACK)]
+        firsts = [bank()[:] for t in range(PACK)]
         for t in range(PACK):
-            skip_pass(skips[t], 0, 0, t, 0)
+            skip_pass(skips[t], 0, 0, CHUNK, t, 0)
         quantize_w1(0, 0)
         gather(1, 0, "v10")
+        gather(1, 1, "v11")
         for t in range(PACK):
-            first_pass(firsts[t], 0, 0, t, 0)
+            first_pass(firsts[t], 0, 0, CHUNK, t, 0)
         for t in range(PACK):
-            skip_pass(skips[t], 0, 0, t, 1)
+            skip_pass(skips[t], 0, 0, CHUNK, t, 1)
         load_w1(1, 0, 60)
         load_w1(1, 1, 68)
         round_w1(0, 1, 0, 320, on_v, "w1_bf01")
         round_w1(0, 1, 320, SPAN, on_s)
         quantize_w1(0, 1)
-        gather(1, 1, "w1_bf01")
         for t in range(PACK):
-            first_pass(firsts[t], 0, 0, t, 1)
+            first_pass(firsts[t], 0, 0, CHUNK, t, 1)
         load_w4(48)
         load_w4_scales(52)
         load_template(0, 12)
         load_template(1, 20)
-        combine(0, 0, 0, firsts[0], skips[0], "w1_bf10")
-        for t in range(1, PACK):
-            combine(0, 0, t, firsts[t], skips[t])
-            round_w1(1, 0, P * (t - 1), P * t, on_s, "w1_bf10")
-        slice_of_h(0, 1, 0, "w1_bf11")
-        round_w1(1, 0, 3 * P, SPAN, on_s)
+        round_w1(1, 0, 0, SPAN, on_v, "w1_bf01")
+        combine(0, 0, CHUNK, 0, firsts[0], skips[0])
         quantize_w1(1, 0)
-        slice_of_h(0, 1, 1)
-        store_h(0, 0, 2, 0, S)
-        round_w1(1, 1, 0, 256, on_v, "w1_bf11")
-        round_w1(1, 1, 256, 384, on_s)
-        slice_of_h(0, 1, 2)
-        round_w1(1, 1, 384, 512, on_s)
+        combine(0, 0, CHUNK, 1, firsts[1], skips[1], "w1_bf11")
+        round_w1(1, 1, 0, 192, on_v, "w1_bf11")
+        round_w1(1, 1, 192, SPAN, on_s)
         quantize_w1(1, 1)
-        slice_of_h(0, 1, 3)
-        store_h(0, 2, 4, 0, S)
+        combine(0, 0, CHUNK, 2, firsts[2], skips[2])
+        combine(0, 0, CHUNK, 3, firsts[3], skips[3])
         for t in range(PACK):
-            slice_of_h(1, 0, t)
+            slice_of_h(0, CHUNK, S, t)
+            if t % 2 == 1:
+                store_h(0, t - 1, t + 1, 0, S)
+        for t in range(PACK):
+            slice_of_h(1, 0, CHUNK, t)
             if t % 2 == 1:
                 store_h(1, t - 1, t + 1, 0, CHUNK)
-            round_part(0, 0, t, "vvss")
-            round_part(0, 1, t, "ssvv")
-        quantize_h(0, 0)
-        quantize_h(0, 1)
-        store_codes(0, 0, S)
-        slice_of_h(1, 1, 0)
-        for t in range(PACK):
-            round_part(1, 0, t, "vvss")
-        slice_of_h(1, 1, 1)
-        store_h(1, 0, 2, CHUNK, S)
-        quantize_h(1, 0)
+            round_h(0, P * t, P * (t + 1), on_s)
+        quantize_h(0, 0, CHUNK)
+        round_h(0, 512, 768, on_v)
+        round_h(1, 0, 256, on_v)
+        round_h(1, 256, 512, on_s)
+        quantize_h(1, 0, CHUNK)
         store_codes(1, 0, CHUNK)
-        slice_of_h(1, 1, 2)
+        round_h(0, 768, 896, on_s)
+        round_h(0, 896, 1024, on_s)
+        for t in range(PACK):
+            slice_of_h(1, 512, 768, t)
+        store_h(1, 0, PACK, 512, 768)
+        quantize_h(0, CHUNK, S)
+        store_codes(0, 0, S)
         sigs = []
         for b in range(N // P):
-            acc = bank()
+            if b % 2 == 0:
+                slice_of_h(1, 768, S, b)
+                slice_of_h(1, 768, S, b + 1)
+            acc = bank()[:]
             for g in range(GROUPS):
-                sig_pass(acc, b, 0, g)
+                sig_pass(acc, b, 0, CHUNK, g, g == 0, g == 1)
             sigs.append(acc)
-            if b == 1:
-                slice_of_h(1, 1, 3)
-                store_h(1, 2, 4, CHUNK, S)
-        misfit(sigs[0], 0, 0)
-        misfit(sigs[1], 1, 0)
-        store_y(0, 2, 0)
-        for t in range(PACK):
-            round_part(1, 1, t, "vvss")
-        misfit(sigs[2], 2, 0)
-        quantize_h(1, 1)
+            if b == 0:
+                round_h(1, 512, 640, on_v)
+                round_h(1, 640, 768, on_s)
+                quantize_h(1, 512, 768)
+        store_h(1, 0, PACK, 768, S)
+        misfit(sigs[0], 0, 1, 0, CHUNK)
+        misfit(sigs[1], 1, 2, 0, CHUNK)
+        store_y(0, 2, 0, CHUNK)
+        round_h(1, 768, 896, on_v)
+        round_h(1, 896, S, on_s)
+        quantize_h(1, 768, S)
         store_codes(1, CHUNK, S)
         store_planes()
-        misfit(sigs[3], 3, 0)
-        store_y(2, 4, 0)
-        sigs = [bank() for b in range(N // P)]
-        for b in range(N // P):
-            sig_pass(sigs[b], b, 1, 0)
-        for b in range(N // P):
-            sig_pass(sigs[b], b, 1, 1)
-            misfit(sigs[b], b, 1)
-            store_y(b, b + 1, 1)
+        misfit(sigs[2], 2, 3, 0, CHUNK)
+        misfit(sigs[3], 3, 4, 0, CHUNK)
+        store_y(2, 4, 0, CHUNK)
+        for lo in (512, 768):
+            pairs = [bank() for u in range(2)]
+            for g in range(GROUPS):
+                for b in range(N // P):
+                    sig_pass(pairs[b // 2][:, 256 * (b % 2) : 256 * (b % 2 + 1)], b, lo, lo + 256, g,
+                             g == 0 and b % 2 == 0, g == 1 and b % 2 == 1)
+            for u in range(2):
+                misfit(pairs[u][:], 2 * u, 2 * u + 2, lo, lo + 256)
+                store_y(2 * u, 2 * u + 2, lo, lo + 256)

@@ -37,7 +37,7 @@ def tile_list_sonar_template_misfit_kernel(
     with ExitStack() as ctx:
         keep = ctx.enter_context(tc.tile_pool(name="keep", bufs=1))
         ring = ctx.enter_context(tc.tile_pool(name="ring", bufs=4))
-        psum = ctx.enter_context(tc.psum_pool(name="psum", bufs=8))
+        psum = ctx.enter_context(tc.psum_pool(name="psum", bufs=1))
         stage = ctx.enter_context(tc.tile_pool(name="stage", bufs=1))
 
         def staged(shape, dtype, name, kib):
@@ -53,7 +53,7 @@ def tile_list_sonar_template_misfit_kernel(
         v_plane = held([P, PASSES, S], U8, "v_plane")
         w3_plane = held([P, PASSES, H], U8, "w3_plane")
         gain = held([P, GROUPS, PACK], F32, "gain")
-        h_plane = held([P, GROUPS, S], U8, "h_plane")
+        h_plane = [held([P, S], U8, f"h_plane{g}") for g in range(GROUPS)]
         tab, w1_raw, w1_bf, w1_codes, w1_plane, w3_raw, w3, w4_plane = {}, {}, {}, {}, {}, {}, {}, {}
         v, h, h_bf, h_codes, template, w4 = {}, {}, {}, {}, {}, {}
         y = held([P, N // P, S], F32, "y")
@@ -66,7 +66,7 @@ def tile_list_sonar_template_misfit_kernel(
             nc.sync.dma_start(tile[0 : PASSES * ROWS, :].bitcast(I32), scales.rearrange("a u n -> u a n").bitcast(I32))
 
         def spread(plane, rows):
-            for q in range(QUADS):
+            for q in (0, 2, 1, 3):
                 nc.sync.dma_start(plane[32 * q : 32 * q + 4].bitcast(I32), rows[8 * q : 8 * q + 8, :].bitcast(I32))
 
         def load_w3():
@@ -101,13 +101,13 @@ def tile_list_sonar_template_misfit_kernel(
             nc.vector.tensor_copy(picked[:], window[:].indirect(offsets[:]))
             spread(v_plane, picked)
 
-        def gather(a, c, name):
-            v[a, c] = held([P, CHUNK], U32, name)
+        def gather(a, c, kib):
+            v[a, c] = staged([P, CHUNK], U32, f"v{a}{c}", kib)
             cols = CHUNK // 16
             nc.vector.tensor_copy(v[a, c][:], tab[a][:].bitcast(U32).indirect(offsets[:, cols * c : cols * (c + 1)]))
 
-        def deal_w3_words(g, copy, name):
-            w3[g] = held([P, PASSES, 2 * SPAN], U8, name)
+        def deal_w3_words(g, copy, kib):
+            w3[g] = staged([P, PASSES, 2 * SPAN], U8, f"w3_{g}", kib)
             copy(
                 w3[g][:].bitcast(U16).rearrange("p a (t m) -> p a t m", t=PACK),
                 w3_raw[0][:].bitcast(U16)[:, :, SPAN * g : SPAN * (g + 1)].rearrange("p a (m t) -> p a t m", t=PACK))
@@ -122,20 +122,20 @@ def tile_list_sonar_template_misfit_kernel(
                 w3_plane[:].rearrange("p a (g t m) -> p (a g) t m", g=GROUPS, t=PACK),
                 w3_rows[:].rearrange("p a (g m t) -> p (a g) t m", g=GROUPS, t=PACK))
 
-        def round_w1(g, a, lo, hi, copy, name=None):
-            if (g, a) not in w1_bf:
-                w1_bf[g, a] = held([P, SPAN * PACK], BF16, name)
-            dealt = w1_bf[g, a][:].rearrange("p (t m i) -> p m i t", t=PACK, i=PACK)
-            copy(dealt[:, lo // PACK : hi // PACK],
-                 w1_raw[g, a][:, :, lo:hi].rearrange("p i (m t) -> p m i t", t=PACK))
+        def round_w1(g, a, t0, t1, copy, rounded):
+            w1_bf[g, a, t0] = rounded
+            dealt = rounded[:].rearrange("p (t m i) -> p m i t", t=t1 - t0, i=PACK)
+            copy(dealt, w1_raw[g, a][:].rearrange("p i (m t) -> p m i t", t=PACK)[:, :, :, t0:t1])
 
-        def quantize_w1(g, a):
-            w1_codes[g, a] = held([P, SPAN], U32, f"w1_codes{g}{a}")
-            w1_plane[g, a] = held([P, SPAN], U8, f"w1_plane{g}{a}")
-            nc.vector.quantize_mx(w1_codes[g, a][:].bitcast(E4M3), w1_plane[g, a][:], w1_bf[g, a][:])
+        def quantize_w1(g, a, t0, t1):
+            if (g, a) not in w1_codes:
+                w1_codes[g, a] = held([P, SPAN], U32, f"w1_codes{g}{a}")
+                w1_plane[g, a] = held([P, SPAN], U8, f"w1_plane{g}{a}")
+            m = slice(P * t0, P * t1)
+            nc.vector.quantize_mx(w1_codes[g, a][:, m].bitcast(E4M3), w1_plane[g, a][:, m], w1_bf[g, a, t0][:])
 
-        def bank():
-            return psum.tile([P, CHUNK], F32, name="bank")
+        def bank(n):
+            return psum.tile([P, CHUNK], F32, name=f"bank{n}")
 
         def picked_operand(a, lo, hi):
             c, at = divmod(lo, CHUNK)
@@ -167,46 +167,49 @@ def tile_list_sonar_template_misfit_kernel(
             rows = out_1[SPAN * g : SPAN * (g + 1), lo:hi].rearrange("(p t) j -> p t j", t=PACK)
             nc.sync.dma_start(rows[:, t0:t1, :], h[g][:, t0:t1, lo:hi])
 
-        def slice_of_h(g, lo, hi, t):
-            if hi - lo == CHUNK:
-                first, skip = bank()[:], bank()[:]
-            else:
-                both = bank()
-                first, skip = both[:, 0 : hi - lo], both[:, hi - lo : 2 * (hi - lo)]
+        def slice_of_h(g, lo, hi, t, name=None):
+            first, skip = bank(2 * t)[:], bank(2 * t + 1)[:]
             for a in range(PASSES):
                 first_pass(first, g, lo, hi, t, a)
             for a in range(PASSES):
                 skip_pass(skip, g, lo, hi, t, a)
-            combine(g, lo, hi, t, first, skip)
+            combine(g, lo, hi, t, first, skip, name)
 
-        def round_h(g, lo, hi, copy):
-            if g not in h_bf:
-                h_bf[g] = held([P, S * PACK], BF16, f"h_bf{g}")
-            dst = h_bf[g][:].rearrange("p (b i t) -> p b t i", i=4, t=PACK)
-            src = h[g][:].rearrange("p t (b i) -> p b t i", i=4)
+        def round_h(g, unit, lo, hi, copy, name=None):
+            if (g, unit) not in h_bf:
+                h_bf[g, unit] = held([P, (unit[1] - unit[0]) * PACK], BF16, name or f"h_bf{g}{unit[0]}")
+            dst = h_bf[g, unit][:].rearrange("p (b i t) -> p b t i", i=4, t=PACK)
+            src = h[g][:, :, unit[0] : unit[1]].rearrange("p t (b i) -> p b t i", i=4)
             copy(dst[:, lo // 4 : hi // 4], src[:, lo // 4 : hi // 4])
 
-        def quantize_h(g, lo, hi):
+        def on_g(out, in_):
+            nc.gpsimd.tensor_scalar(out, in_, 1.0, 0.0, ALU.mult, ALU.add)
+
+        def round_h_pool(g, unit, lo, hi):
+            if (g, unit) not in h_bf:
+                h_bf[g, unit] = held([P, (unit[1] - unit[0]) * PACK], BF16, f"h_bf{g}{unit[0]}")
+            dst = h_bf[g, unit][:].rearrange("p (j t) -> p j t", t=PACK)
+            on_g(dst[:, lo:hi], h[g][:, :, unit[0] : unit[1]].rearrange("p t j -> p j t")[:, lo:hi])
+
+        def quantize_h(g, unit):
+            lo, hi = unit
             if g not in h_codes:
                 h_codes[g] = held([P, S], U32, f"h_codes{g}")
-            nc.vector.quantize_mx(
-                h_codes[g][:, lo:hi].bitcast(E4M3), h_plane[H_ROW:P, g, lo:hi], h_bf[g][:, PACK * lo : PACK * hi])
+            nc.vector.quantize_mx(h_codes[g][:, lo:hi].bitcast(E4M3), h_plane[g][H_ROW:P, lo:hi], h_bf[g, unit][:])
 
         def store_codes(g, lo, hi):
             nc.sync.dma_start(
                 out_2[g].rearrange("p m t -> p (m t)").bitcast(I32)[:, lo:hi], h_codes[g][:, lo:hi].bitcast(I32))
 
-        def store_planes():
+        def store_planes(g):
             for r in range(QUADS):
-                nc.sync.dma_start(
-                    out_3[:, r::4, :].rearrange("g q m -> q g m").bitcast(I32),
-                    h_plane[H_ROW + r : P : 32].bitcast(I32))
+                nc.sync.dma_start(out_3[g, r::4, :].bitcast(I32), h_plane[g][H_ROW + r : P : 32, :].bitcast(I32))
 
         def sig_pass(acc, b, lo, hi, g, start, stop):
             m = slice(P * b, P * (b + 1))
             nc.tensor.matmul_mx(
                 acc, w4[0][:, g, m].bitcast(E4M3), w4_plane[0][W4_ROW:P, g, m],
-                h_codes[g][:, lo:hi].bitcast(E4M3), h_plane[H_ROW:P, g, lo:hi], start=start, stop=stop)
+                h_codes[g][:, lo:hi].bitcast(E4M3), h_plane[g][H_ROW:P, lo:hi], start=start, stop=stop)
 
         def misfit(acc, b0, b1, lo, hi):
             n = b1 - b0
@@ -237,98 +240,103 @@ def tile_list_sonar_template_misfit_kernel(
         load_w3()
         load_w1(0, 0, 48)
         gather_planes()
-        load_tab(1, 24)
         load_w1(0, 1, 16)
-        gather(0, 0, "v00")
+        load_tab(1, 24)
+        gather(0, 0, 88)
         deal_w3_plane()
-        gather(0, 1, "v01")
-        deal_w3_words(0, on_s, "w3_0")
-        round_w1(0, 0, 0, SPAN, on_act, "w1_bf00")
-        deal_w3_words(1, on_s, "w3_1")
-        skips = [bank()[:] for t in range(PACK)]
-        firsts = [bank()[:] for t in range(PACK)]
-        for t in range(PACK):
-            skip_pass(skips[t], 0, 0, CHUNK, t, 0)
-        quantize_w1(0, 0)
-        gather(1, 0, "v10")
-        gather(1, 1, "v11")
+        gather(0, 1, 90)
+        deal_w3_words(1, on_s, 80)
+        round_w1(0, 0, 0, PACK, on_act, staged([P, SPAN * PACK], BF16, "w1_bf00", 84))
+        deal_w3_words(0, on_s, 54)
+        pairs = [(bank(2 * t)[:], bank(2 * t + 1)[:]) for t in range(PACK)]
+        firsts = [pair[0] for pair in pairs]
+        skips = [pair[1] for pair in pairs]
+        quantize_w1(0, 0, 0, PACK)
         for t in range(PACK):
             first_pass(firsts[t], 0, 0, CHUNK, t, 0)
         for t in range(PACK):
-            skip_pass(skips[t], 0, 0, CHUNK, t, 1)
+            skip_pass(skips[t], 0, 0, CHUNK, t, 0)
         load_w1(1, 0, 60)
         load_w1(1, 1, 68)
-        round_w1(0, 1, 0, 320, on_v, "w1_bf01")
-        round_w1(0, 1, 320, SPAN, on_s)
-        quantize_w1(0, 1)
+        round_w1(0, 1, 0, PACK, on_v, staged([P, SPAN * PACK], BF16, "w1_bf01", 84))
+        quantize_w1(0, 1, 0, PACK)
+        gather(1, 0, 84)
         for t in range(PACK):
             first_pass(firsts[t], 0, 0, CHUNK, t, 1)
+            skip_pass(skips[t], 0, 0, CHUNK, t, 1)
+        gather(1, 1, 86)
         load_w4(48)
         load_w4_scales(52)
         load_template(0, 12)
         load_template(1, 20)
-        round_w1(1, 0, 0, SPAN, on_v, "w1_bf01")
-        combine(0, 0, CHUNK, 0, firsts[0], skips[0])
-        quantize_w1(1, 0)
-        combine(0, 0, CHUNK, 1, firsts[1], skips[1], "w1_bf11")
-        round_w1(1, 1, 0, 192, on_v, "w1_bf11")
-        round_w1(1, 1, 192, SPAN, on_s)
-        quantize_w1(1, 1)
-        combine(0, 0, CHUNK, 2, firsts[2], skips[2])
+        round_w1(1, 0, 0, 2, on_v, staged([P, SPAN * 2], BF16, "w1_bf10", 30))
+        combine(0, 0, CHUNK, 0, firsts[0], skips[0], "lent0")
+        quantize_w1(1, 0, 0, 2)
+        combine(0, 0, CHUNK, 1, firsts[1], skips[1], "lent1")
+        combine(0, 0, CHUNK, 2, firsts[2], skips[2], "lent2")
+        round_w1(1, 0, 2, 4, on_s, held([P, SPAN * 2], BF16, "lent0"))
+        round_w1(1, 1, 0, 2, on_v, held([P, SPAN * 2], BF16, "lent2"))
         combine(0, 0, CHUNK, 3, firsts[3], skips[3])
-        for t in range(PACK):
+        round_w1(1, 1, 2, 4, on_s, held([P, SPAN * 2], BF16, "lent1"))
+        quantize_w1(1, 0, 2, 4)
+        quantize_w1(1, 1, 0, 2)
+        slice_of_h(0, CHUNK, S, 0)
+        quantize_w1(1, 1, 2, 4)
+        for t in range(1, PACK):
             slice_of_h(0, CHUNK, S, t)
             if t % 2 == 1:
                 store_h(0, t - 1, t + 1, 0, S)
+        low, high = (0, CHUNK), (CHUNK, S)
         for t in range(PACK):
+            round_h(0, low, P * t, P * (t + 1), on_s if t < 1 else on_v)
             slice_of_h(1, 0, CHUNK, t)
             if t % 2 == 1:
                 store_h(1, t - 1, t + 1, 0, CHUNK)
-            round_h(0, P * t, P * (t + 1), on_s)
-        quantize_h(0, 0, CHUNK)
-        round_h(0, 512, 768, on_v)
-        round_h(1, 0, 256, on_v)
-        round_h(1, 256, 512, on_s)
-        quantize_h(1, 0, CHUNK)
+        quantize_h(0, low)
+        store_codes(0, 0, CHUNK)
+        round_h(1, low, 0, 320, on_s)
+        round_h(1, low, 320, 512, on_v)
+        slice_of_h(1, CHUNK, S, 0)
+        quantize_h(1, low)
         store_codes(1, 0, CHUNK)
-        round_h(0, 768, 896, on_s)
-        round_h(0, 896, 1024, on_s)
+        slice_of_h(1, CHUNK, S, 1)
+        store_h(1, 0, 2, CHUNK, S)
+        slice_of_h(1, CHUNK, S, 2)
         for t in range(PACK):
-            slice_of_h(1, 512, 768, t)
-        store_h(1, 0, PACK, 512, 768)
-        quantize_h(0, CHUNK, S)
-        store_codes(0, 0, S)
-        sigs = []
+            round_h(0, high, P * t, P * (t + 1), on_s if t < 3 else on_v)
+        first, skip = bank(6)[:], bank(7)[:]
+        for a in range(PASSES):
+            first_pass(first, 1, CHUNK, S, 3, a)
+        for a in range(PASSES):
+            skip_pass(skip, 1, CHUNK, S, 3, a)
+        sigs = [bank(b)[:] for b in range(N // P)]
         for b in range(N // P):
-            if b % 2 == 0:
-                slice_of_h(1, 768, S, b)
-                slice_of_h(1, 768, S, b + 1)
-            acc = bank()[:]
             for g in range(GROUPS):
-                sig_pass(acc, b, 0, CHUNK, g, g == 0, g == 1)
-            sigs.append(acc)
-            if b == 0:
-                round_h(1, 512, 640, on_v)
-                round_h(1, 640, 768, on_s)
-                quantize_h(1, 512, 768)
-        store_h(1, 0, PACK, 768, S)
+                sig_pass(sigs[b], b, 0, CHUNK, g, g == 0, g == 1)
+        th = ring.tile([P, CHUNK], F32, name="th")
+        nc.scalar.activation(th[:], first, ACT.Tanh)
         misfit(sigs[0], 0, 1, 0, CHUNK)
+        store_y(0, 1, 0, CHUNK)
+        nc.vector.scalar_tensor_tensor(h[1][:, 3, CHUNK:S], th[:], gain[:, 1, 3:4], skip, ALU.mult, ALU.add)
+        store_h(1, 2, 4, CHUNK, S)
         misfit(sigs[1], 1, 2, 0, CHUNK)
-        store_y(0, 2, 0, CHUNK)
-        round_h(1, 768, 896, on_v)
-        round_h(1, 896, S, on_s)
-        quantize_h(1, 768, S)
-        store_codes(1, CHUNK, S)
-        store_planes()
+        store_y(1, 2, 0, CHUNK)
+        round_h(1, high, 0, 256, on_s)
+        round_h(1, high, 256, 512, on_v)
         misfit(sigs[2], 2, 3, 0, CHUNK)
+        store_y(2, 3, 0, CHUNK)
+        quantize_h(0, high)
+        quantize_h(1, high)
+        sigs += [bank(4 + b)[:] for b in range(N // P)]
+        for g in range(GROUPS):
+            for b in range(N // P):
+                sig_pass(sigs[4 + b], b, CHUNK, S, g, g == 0, g == 1)
         misfit(sigs[3], 3, 4, 0, CHUNK)
-        store_y(2, 4, 0, CHUNK)
-        for lo in (512, 768):
-            pairs = [bank() for u in range(2)]
-            for g in range(GROUPS):
-                for b in range(N // P):
-                    sig_pass(pairs[b // 2][:, 256 * (b % 2) : 256 * (b % 2 + 1)], b, lo, lo + 256, g,
-                             g == 0 and b % 2 == 0, g == 1 and b % 2 == 1)
-            for u in range(2):
-                misfit(pairs[u][:], 2 * u, 2 * u + 2, lo, lo + 256)
-                store_y(2 * u, 2 * u + 2, lo, lo + 256)
+        store_y(3, 4, 0, CHUNK)
+        store_codes(0, CHUNK, S)
+        store_planes(0)
+        store_codes(1, CHUNK, S)
+        store_planes(1)
+        for b in range(N // P):
+            misfit(sigs[4 + b], b, b + 1, CHUNK, S)
+            store_y(b, b + 1, CHUNK, S)

@@ -41,7 +41,7 @@ def tile_list_sonar_template_misfit_kernel(
         stage = ctx.enter_context(tc.tile_pool(name="stage", bufs=1))
 
         def staged(shape, dtype, name, kib):
-            return stage.tile(shape, dtype, name=name, align_bytes=64, offset=1024 * kib)
+            return stage.tile(shape, dtype, name=name, align_bytes=64, offset=int(1024 * kib))
 
         def held(shape, dtype, name):
             return keep.tile(shape, dtype, name=name, align_bytes=64)
@@ -50,10 +50,10 @@ def tile_list_sonar_template_misfit_kernel(
         window = staged([P, T], U8, "window", 23)
         w3_rows = held([P, PASSES, H], U8, "w3_rows")
         picked = held([P, S], U8, "picked")
-        v_plane = held([P, PASSES, S], U8, "v_plane")
+        v_plane = [held([P, S], U8, f"v_plane{a}") for a in range(PASSES)]
         w3_plane = held([P, PASSES, H], U8, "w3_plane")
-        gain = held([P, GROUPS, PACK], F32, "gain")
-        h_plane = [held([P, S], U8, f"h_plane{g}") for g in range(GROUPS)]
+        gain = staged([P, GROUPS, PACK], F32, "gain", 23.5)
+        h_plane = [held([P, GROUPS, CHUNK], U8, f"h_plane{c}") for c in range(CHUNKS)]
         tab, w1_raw, w1_bf, w1_codes, w1_plane, w3_raw, w3, w4_plane = {}, {}, {}, {}, {}, {}, {}, {}
         v, h, h_bf, h_codes, template, w4 = {}, {}, {}, {}, {}, {}
         y = held([P, N // P, S], F32, "y")
@@ -65,9 +65,10 @@ def tile_list_sonar_template_misfit_kernel(
         def load_rows(tile, scales):
             nc.sync.dma_start(tile[0 : PASSES * ROWS, :].bitcast(I32), scales.rearrange("a u n -> u a n").bitcast(I32))
 
-        def spread(plane, rows):
+        def spread(a):
             for q in (0, 2, 1, 3):
-                nc.sync.dma_start(plane[32 * q : 32 * q + 4].bitcast(I32), rows[8 * q : 8 * q + 8, :].bitcast(I32))
+                nc.sync.dma_start(
+                    v_plane[a][32 * q : 32 * q + 4, :].bitcast(I32), picked[8 * q + a : 8 * q + 8 : 2, :].bitcast(I32))
 
         def load_w3():
             w3_raw[0] = held([P, PASSES, 2 * H // 4], I32, "w3_raw")
@@ -99,7 +100,6 @@ def tile_list_sonar_template_misfit_kernel(
 
         def gather_planes():
             nc.vector.tensor_copy(picked[:], window[:].indirect(offsets[:]))
-            spread(v_plane, picked)
 
         def gather(a, c, kib):
             v[a, c] = staged([P, CHUNK], U32, f"v{a}{c}", kib)
@@ -139,7 +139,7 @@ def tile_list_sonar_template_misfit_kernel(
 
         def picked_operand(a, lo, hi):
             c, at = divmod(lo, CHUNK)
-            return v[a, c][:, at : at + hi - lo].bitcast(E4M3), v_plane[:, a, lo:hi]
+            return v[a, c][:, at : at + hi - lo].bitcast(E4M3), v_plane[a][:, lo:hi]
 
         def first_pass(acc, g, lo, hi, t, a):
             m = slice(P * t, P * (t + 1))
@@ -195,21 +195,23 @@ def tile_list_sonar_template_misfit_kernel(
             lo, hi = unit
             if g not in h_codes:
                 h_codes[g] = held([P, S], U32, f"h_codes{g}")
-            nc.vector.quantize_mx(h_codes[g][:, lo:hi].bitcast(E4M3), h_plane[g][H_ROW:P, lo:hi], h_bf[g, unit][:])
+            nc.vector.quantize_mx(h_codes[g][:, lo:hi].bitcast(E4M3), h_plane[lo // CHUNK][H_ROW:P, g, :], h_bf[g, unit][:])
 
         def store_codes(g, lo, hi):
             nc.sync.dma_start(
                 out_2[g].rearrange("p m t -> p (m t)").bitcast(I32)[:, lo:hi], h_codes[g][:, lo:hi].bitcast(I32))
 
-        def store_planes(g):
+        def store_planes(c):
             for r in range(QUADS):
-                nc.sync.dma_start(out_3[g, r::4, :].bitcast(I32), h_plane[g][H_ROW + r : P : 32, :].bitcast(I32))
+                nc.sync.dma_start(
+                    out_3[:, r::4, CHUNK * c : CHUNK * (c + 1)].rearrange("g q m -> q g m").bitcast(I32),
+                    h_plane[c][H_ROW + r : P : 32].bitcast(I32))
 
         def sig_pass(acc, b, lo, hi, g, start, stop):
             m = slice(P * b, P * (b + 1))
             nc.tensor.matmul_mx(
                 acc, w4[0][:, g, m].bitcast(E4M3), w4_plane[0][W4_ROW:P, g, m],
-                h_codes[g][:, lo:hi].bitcast(E4M3), h_plane[g][H_ROW:P, lo:hi], start=start, stop=stop)
+                h_codes[g][:, lo:hi].bitcast(E4M3), h_plane[lo // CHUNK][H_ROW:P, g, :], start=start, stop=stop)
 
         def misfit(acc, b0, b1, lo, hi):
             n = b1 - b0
@@ -231,45 +233,50 @@ def tile_list_sonar_template_misfit_kernel(
         nc.vector.memset(w3_rows[:].rearrange("p a n -> p (a n)").bitcast(I32), 0)
         nc.vector.memset(window[32:64, :].bitcast(I32), 0)
         nc.vector.memset(window[64:P, :].bitcast(I32), 0)
-        nc.vector.memset(v_plane[:].rearrange("p a n -> p (a n)").bitcast(I32), 0)
+        for a in range(PASSES):
+            nc.vector.memset(v_plane[a][:].bitcast(I32), 0)
         load_rows(window, tab_scales)
         nc.sync.dma_start(offsets[:], offs)
-        load_gain()
         load_tab(0, 64)
         load_w3_scales()
         load_w3()
         load_w1(0, 0, 48)
         gather_planes()
-        load_w1(0, 1, 16)
+        spread(0)
+        load_w1(0, 1, 15.5)
         load_tab(1, 24)
-        gather(0, 0, 88)
+        spread(1)
+        load_gain()
+        gather(0, 0, 90)
         deal_w3_plane()
-        gather(0, 1, 90)
+        gather(0, 1, 92)
         deal_w3_words(1, on_s, 80)
-        round_w1(0, 0, 0, PACK, on_act, staged([P, SPAN * PACK], BF16, "w1_bf00", 84))
-        deal_w3_words(0, on_s, 54)
         pairs = [(bank(2 * t)[:], bank(2 * t + 1)[:]) for t in range(PACK)]
         firsts = [pair[0] for pair in pairs]
         skips = [pair[1] for pair in pairs]
-        quantize_w1(0, 0, 0, PACK)
+        for a in range(PASSES):
+            round_w1(0, a, 0, 2, on_v, staged([P, SPAN * 2], BF16, f"w1_bf0{a}a", 84))
+            round_w1(0, a, 2, 4, on_act, staged([P, SPAN * 2], BF16, f"w1_bf0{a}b", 86))
+            quantize_w1(0, a, 0, 2)
+            quantize_w1(0, a, 2, 4)
+            if a == 0:
+                deal_w3_words(0, on_s, 54)
+        load_w1(1, 0, 60)
+        load_w1(1, 1, 68)
         for t in range(PACK):
             first_pass(firsts[t], 0, 0, CHUNK, t, 0)
         for t in range(PACK):
             skip_pass(skips[t], 0, 0, CHUNK, t, 0)
-        load_w1(1, 0, 60)
-        load_w1(1, 1, 68)
-        round_w1(0, 1, 0, PACK, on_v, staged([P, SPAN * PACK], BF16, "w1_bf01", 84))
-        quantize_w1(0, 1, 0, PACK)
-        gather(1, 0, 84)
+        gather(1, 0, 85)
         for t in range(PACK):
             first_pass(firsts[t], 0, 0, CHUNK, t, 1)
             skip_pass(skips[t], 0, 0, CHUNK, t, 1)
-        gather(1, 1, 86)
+        gather(1, 1, 87)
         load_w4(48)
         load_w4_scales(52)
-        load_template(0, 12)
-        load_template(1, 20)
-        round_w1(1, 0, 0, 2, on_v, staged([P, SPAN * 2], BF16, "w1_bf10", 30))
+        load_template(0, 8)
+        load_template(1, 28)
+        round_w1(1, 0, 0, 2, on_v, staged([P, SPAN * 2], BF16, "w1_bf10", 24))
         combine(0, 0, CHUNK, 0, firsts[0], skips[0], "lent0")
         quantize_w1(1, 0, 0, 2)
         combine(0, 0, CHUNK, 1, firsts[1], skips[1], "lent1")
@@ -299,28 +306,22 @@ def tile_list_sonar_template_misfit_kernel(
         slice_of_h(1, CHUNK, S, 0)
         quantize_h(1, low)
         store_codes(1, 0, CHUNK)
+        store_planes(0)
         slice_of_h(1, CHUNK, S, 1)
         store_h(1, 0, 2, CHUNK, S)
         slice_of_h(1, CHUNK, S, 2)
         for t in range(PACK):
             round_h(0, high, P * t, P * (t + 1), on_s if t < 3 else on_v)
-        first, skip = bank(6)[:], bank(7)[:]
-        for a in range(PASSES):
-            first_pass(first, 1, CHUNK, S, 3, a)
-        for a in range(PASSES):
-            skip_pass(skip, 1, CHUNK, S, 3, a)
         sigs = [bank(b)[:] for b in range(N // P)]
         for b in range(N // P):
             for g in range(GROUPS):
                 sig_pass(sigs[b], b, 0, CHUNK, g, g == 0, g == 1)
-        th = ring.tile([P, CHUNK], F32, name="th")
-        nc.scalar.activation(th[:], first, ACT.Tanh)
-        misfit(sigs[0], 0, 1, 0, CHUNK)
-        store_y(0, 1, 0, CHUNK)
-        nc.vector.scalar_tensor_tensor(h[1][:, 3, CHUNK:S], th[:], gain[:, 1, 3:4], skip, ALU.mult, ALU.add)
-        store_h(1, 2, 4, CHUNK, S)
-        misfit(sigs[1], 1, 2, 0, CHUNK)
-        store_y(1, 2, 0, CHUNK)
+            if b < 2:
+                misfit(sigs[b], b, b + 1, 0, CHUNK)
+                store_y(b, b + 1, 0, CHUNK)
+            if b == 1:
+                slice_of_h(1, CHUNK, S, 3)
+                store_h(1, 2, 4, CHUNK, S)
         round_h(1, high, 0, 256, on_s)
         round_h(1, high, 256, 512, on_v)
         misfit(sigs[2], 2, 3, 0, CHUNK)
@@ -334,7 +335,6 @@ def tile_list_sonar_template_misfit_kernel(
         misfit(sigs[3], 3, 4, 0, CHUNK)
         store_y(3, 4, 0, CHUNK)
         store_codes(0, CHUNK, S)
-        store_planes(0)
         store_codes(1, CHUNK, S)
         store_planes(1)
         for b in range(N // P):

@@ -53,9 +53,10 @@ def tile_list_sonar_template_misfit_kernel(
         v_plane = [held([P, S], U8, f"v_plane{a}") for a in range(PASSES)]
         w3_plane = held([P, PASSES, H], U8, "w3_plane")
         gain = staged([P, GROUPS, PACK], F32, "gain", 23.5)
-        h_plane = [held([P, GROUPS, CHUNK], U8, f"h_plane{c}") for c in range(CHUNKS)]
+        h_plane = held([P, GROUPS, S], U8, "h_plane")
+        h_codes = [held([P, GROUPS, CHUNK], U32, f"h_codes{c}") for c in range(CHUNKS)]
         tab, w1_raw, w1_bf, w1_codes, w1_plane, w3_raw, w3, w4_plane = {}, {}, {}, {}, {}, {}, {}, {}
-        v, h, h_bf, h_codes, template, w4 = {}, {}, {}, {}, {}, {}
+        v, h, h_bf, template, w4 = {}, {}, {}, {}, {}
         y = held([P, N // P, S], F32, "y")
 
         def load_tab(a, kib):
@@ -122,7 +123,8 @@ def tile_list_sonar_template_misfit_kernel(
                 w3_plane[:].rearrange("p a (g t m) -> p (a g) t m", g=GROUPS, t=PACK),
                 w3_rows[:].rearrange("p a (g m t) -> p (a g) t m", g=GROUPS, t=PACK))
 
-        def round_w1(g, a, t0, t1, copy, rounded):
+        def round_w1(g, a, t0, t1, copy, kib):
+            rounded = staged([P, (t1 - t0) * SPAN], BF16, f"w1_bf{g}{a}{t0}", kib)
             w1_bf[g, a, t0] = rounded
             dealt = rounded[:].rearrange("p (t m i) -> p m i t", t=t1 - t0, i=PACK)
             copy(dealt, w1_raw[g, a][:].rearrange("p i (m t) -> p m i t", t=PACK)[:, :, :, t0:t1])
@@ -153,13 +155,13 @@ def tile_list_sonar_template_misfit_kernel(
                 acc, w3[g][:, a, 2 * P * t : 2 * P * (t + 1)].bitcast(E2M1), w3_plane[:, a, at : at + P],
                 *picked_operand(a, lo, hi), start=(a == 0), stop=(a == PASSES - 1))
 
-        def combine(g, lo, hi, t, first, skip, name=None):
+        def combine(g, lo, hi, t, first, skip, kib=None):
             if g not in h:
                 h[g] = held([P, PACK, S], F32, f"h{g}")
-            if name is None:
+            if kib is None:
                 th = ring.tile([P, hi - lo], F32, name="th")
             else:
-                th = held([P, hi - lo], F32, name)
+                th = staged([P, hi - lo], F32, f"th{t}", kib)
             nc.scalar.activation(th[:], first, ACT.Tanh)
             nc.vector.scalar_tensor_tensor(h[g][:, t, lo:hi], th[:], gain[:, g, t : t + 1], skip, ALU.mult, ALU.add)
 
@@ -167,13 +169,13 @@ def tile_list_sonar_template_misfit_kernel(
             rows = out_1[SPAN * g : SPAN * (g + 1), lo:hi].rearrange("(p t) j -> p t j", t=PACK)
             nc.sync.dma_start(rows[:, t0:t1, :], h[g][:, t0:t1, lo:hi])
 
-        def slice_of_h(g, lo, hi, t, name=None):
+        def slice_of_h(g, lo, hi, t):
             first, skip = bank(2 * t)[:], bank(2 * t + 1)[:]
             for a in range(PASSES):
                 first_pass(first, g, lo, hi, t, a)
             for a in range(PASSES):
                 skip_pass(skip, g, lo, hi, t, a)
-            combine(g, lo, hi, t, first, skip, name)
+            combine(g, lo, hi, t, first, skip)
 
         def round_h(g, unit, lo, hi, copy, name=None):
             if (g, unit) not in h_bf:
@@ -193,25 +195,24 @@ def tile_list_sonar_template_misfit_kernel(
 
         def quantize_h(g, unit):
             lo, hi = unit
-            if g not in h_codes:
-                h_codes[g] = held([P, S], U32, f"h_codes{g}")
-            nc.vector.quantize_mx(h_codes[g][:, lo:hi].bitcast(E4M3), h_plane[lo // CHUNK][H_ROW:P, g, :], h_bf[g, unit][:])
+            nc.vector.quantize_mx(
+                h_codes[lo // CHUNK][:, g, :].bitcast(E4M3), h_plane[H_ROW:P, g, lo:hi], h_bf[g, unit][:])
 
-        def store_codes(g, lo, hi):
-            nc.sync.dma_start(
-                out_2[g].rearrange("p m t -> p (m t)").bitcast(I32)[:, lo:hi], h_codes[g][:, lo:hi].bitcast(I32))
+        def store_codes(c, g0, g1):
+            words = out_2.rearrange("g p m t -> p g (m t)").bitcast(I32)
+            nc.sync.dma_start(words[:, g0:g1, CHUNK * c : CHUNK * (c + 1)], h_codes[c][:, g0:g1].bitcast(I32))
 
-        def store_planes(c):
+        def store_planes():
             for r in range(QUADS):
                 nc.sync.dma_start(
-                    out_3[:, r::4, CHUNK * c : CHUNK * (c + 1)].rearrange("g q m -> q g m").bitcast(I32),
-                    h_plane[c][H_ROW + r : P : 32].bitcast(I32))
+                    out_3[:, r::4, :].rearrange("g q m -> q g m").bitcast(I32),
+                    h_plane[H_ROW + r : P : 32].bitcast(I32))
 
         def sig_pass(acc, b, lo, hi, g, start, stop):
             m = slice(P * b, P * (b + 1))
             nc.tensor.matmul_mx(
                 acc, w4[0][:, g, m].bitcast(E4M3), w4_plane[0][W4_ROW:P, g, m],
-                h_codes[g][:, lo:hi].bitcast(E4M3), h_plane[lo // CHUNK][H_ROW:P, g, :], start=start, stop=stop)
+                h_codes[lo // CHUNK][:, g, :].bitcast(E4M3), h_plane[H_ROW:P, g, lo:hi], start=start, stop=stop)
 
         def misfit(acc, b0, b1, lo, hi):
             n = b1 - b0
@@ -255,8 +256,8 @@ def tile_list_sonar_template_misfit_kernel(
         firsts = [pair[0] for pair in pairs]
         skips = [pair[1] for pair in pairs]
         for a in range(PASSES):
-            round_w1(0, a, 0, 2, on_v, staged([P, SPAN * 2], BF16, f"w1_bf0{a}a", 84))
-            round_w1(0, a, 2, 4, on_act, staged([P, SPAN * 2], BF16, f"w1_bf0{a}b", 86))
+            round_w1(0, a, 0, 2, on_v, 84)
+            round_w1(0, a, 2, 4, on_act, 86)
             quantize_w1(0, a, 0, 2)
             quantize_w1(0, a, 2, 4)
             if a == 0:
@@ -276,18 +277,18 @@ def tile_list_sonar_template_misfit_kernel(
         load_w4_scales(52)
         load_template(0, 8)
         load_template(1, 28)
-        round_w1(1, 0, 0, 2, on_v, staged([P, SPAN * 2], BF16, "w1_bf10", 24))
-        combine(0, 0, CHUNK, 0, firsts[0], skips[0], "lent0")
+        combine(0, 0, CHUNK, 0, firsts[0], skips[0], 100)
+        round_w1(1, 0, 0, 2, on_v, 99)
+        combine(0, 0, CHUNK, 1, firsts[1], skips[1], 104)
         quantize_w1(1, 0, 0, 2)
-        combine(0, 0, CHUNK, 1, firsts[1], skips[1], "lent1")
-        combine(0, 0, CHUNK, 2, firsts[2], skips[2], "lent2")
-        round_w1(1, 0, 2, 4, on_s, held([P, SPAN * 2], BF16, "lent0"))
-        round_w1(1, 1, 0, 2, on_v, held([P, SPAN * 2], BF16, "lent2"))
+        combine(0, 0, CHUNK, 2, firsts[2], skips[2], 106)
+        round_w1(1, 0, 2, 4, on_s, 101)
         combine(0, 0, CHUNK, 3, firsts[3], skips[3])
-        round_w1(1, 1, 2, 4, on_s, held([P, SPAN * 2], BF16, "lent1"))
+        round_w1(1, 1, 0, 2, on_v, 106)
+        round_w1(1, 1, 2, 4, on_s, 104)
         quantize_w1(1, 0, 2, 4)
-        quantize_w1(1, 1, 0, 2)
         slice_of_h(0, CHUNK, S, 0)
+        quantize_w1(1, 1, 0, 2)
         quantize_w1(1, 1, 2, 4)
         for t in range(1, PACK):
             slice_of_h(0, CHUNK, S, t)
@@ -300,13 +301,11 @@ def tile_list_sonar_template_misfit_kernel(
             if t % 2 == 1:
                 store_h(1, t - 1, t + 1, 0, CHUNK)
         quantize_h(0, low)
-        store_codes(0, 0, CHUNK)
         round_h(1, low, 0, 320, on_s)
         round_h(1, low, 320, 512, on_v)
         slice_of_h(1, CHUNK, S, 0)
         quantize_h(1, low)
-        store_codes(1, 0, CHUNK)
-        store_planes(0)
+        store_codes(0, 0, 2)
         slice_of_h(1, CHUNK, S, 1)
         store_h(1, 0, 2, CHUNK, S)
         slice_of_h(1, CHUNK, S, 2)
@@ -325,18 +324,17 @@ def tile_list_sonar_template_misfit_kernel(
         round_h(1, high, 0, 256, on_s)
         round_h(1, high, 256, 512, on_v)
         misfit(sigs[2], 2, 3, 0, CHUNK)
-        store_y(2, 3, 0, CHUNK)
         quantize_h(0, high)
+        store_codes(1, 0, 1)
         quantize_h(1, high)
         sigs += [bank(4 + b)[:] for b in range(N // P)]
         for g in range(GROUPS):
             for b in range(N // P):
                 sig_pass(sigs[4 + b], b, CHUNK, S, g, g == 0, g == 1)
         misfit(sigs[3], 3, 4, 0, CHUNK)
-        store_y(3, 4, 0, CHUNK)
-        store_codes(0, CHUNK, S)
-        store_codes(1, CHUNK, S)
-        store_planes(1)
+        store_y(2, 4, 0, CHUNK)
+        store_codes(1, 1, 2)
+        store_planes()
         for b in range(N // P):
             misfit(sigs[4 + b], b, b + 1, CHUNK, S)
             store_y(b, b + 1, CHUNK, S)

@@ -184,15 +184,6 @@ def tile_list_sonar_template_misfit_kernel(
             src = h[g][:, :, unit[0] : unit[1]].rearrange("p t (b i) -> p b t i", i=4)
             copy(dst[:, lo // 4 : hi // 4], src[:, lo // 4 : hi // 4])
 
-        def on_g(out, in_):
-            nc.gpsimd.tensor_scalar(out, in_, 1.0, 0.0, ALU.mult, ALU.add)
-
-        def round_h_pool(g, unit, lo, hi):
-            if (g, unit) not in h_bf:
-                h_bf[g, unit] = held([P, (unit[1] - unit[0]) * PACK], BF16, f"h_bf{g}{unit[0]}")
-            dst = h_bf[g, unit][:].rearrange("p (j t) -> p j t", t=PACK)
-            on_g(dst[:, lo:hi], h[g][:, :, unit[0] : unit[1]].rearrange("p t j -> p j t")[:, lo:hi])
-
         def quantize_h(g, unit):
             lo, hi = unit
             nc.vector.quantize_mx(
@@ -214,9 +205,12 @@ def tile_list_sonar_template_misfit_kernel(
                 acc, w4[0][:, g, m].bitcast(E4M3), w4_plane[0][W4_ROW:P, g, m],
                 h_codes[lo // CHUNK][:, g, :].bitcast(E4M3), h_plane[H_ROW:P, g, lo:hi], start=start, stop=stop)
 
-        def misfit(acc, b0, b1, lo, hi):
+        def misfit(acc, b0, b1, lo, hi, name=None):
             n = b1 - b0
-            diff = ring.tile([P, n, hi - lo], F32, name="diff")
+            if name is None:
+                diff = ring.tile([P, n, hi - lo], F32, name="diff")
+            else:
+                diff = held([P, n, hi - lo], F32, name)
             nc.vector.tensor_tensor(
                 diff[:], template[b0 // 2][:, b0 % 2 : b0 % 2 + n, lo:hi],
                 acc.rearrange("p (b j) -> p b j", b=n), ALU.subtract)
@@ -243,8 +237,8 @@ def tile_list_sonar_template_misfit_kernel(
         load_w3()
         load_w1(0, 0, 48)
         gather_planes()
-        spread(0)
         load_w1(0, 1, 15.5)
+        spread(0)
         load_tab(1, 24)
         spread(1)
         load_gain()

@@ -290,16 +290,16 @@ def tile_list_sonar_template_misfit_kernel(
                 store_h(0, t - 1, t + 1, 0, S)
         low, high = (0, CHUNK), (CHUNK, S)
         for t in range(PACK):
-            round_h(0, low, P * t, P * (t + 1), on_s if t < 1 else on_v)
+            round_h(0, low, P * t, P * (t + 1), on_s if t < 2 else on_v)
             slice_of_h(1, 0, CHUNK, t)
             if t % 2 == 1:
                 store_h(1, t - 1, t + 1, 0, CHUNK)
         quantize_h(0, low)
-        round_h(1, low, 0, 320, on_s)
-        round_h(1, low, 320, 512, on_v)
-        slice_of_h(1, CHUNK, S, 0)
+        round_h(1, low, 0, 192, on_s)
+        round_h(1, low, 192, 512, on_v)
         quantize_h(1, low)
         store_codes(0, 0, 2)
+        slice_of_h(1, CHUNK, S, 0)
         slice_of_h(1, CHUNK, S, 1)
         store_h(1, 0, 2, CHUNK, S)
         slice_of_h(1, CHUNK, S, 2)

@@ -53,7 +53,7 @@ def tile_list_sonar_template_misfit_kernel(
         v_plane = [held([P, S], U8, f"v_plane{a}") for a in range(PASSES)]
         w3_plane = held([P, PASSES, H], U8, "w3_plane")
         gain = staged([P, GROUPS, PACK], F32, "gain", 23.5)
-        h_plane = held([P, GROUPS, S], U8, "h_plane")
+        h_plane = [held([P, GROUPS, CHUNK], U8, f"h_plane{c}") for c in range(CHUNKS)]
         h_codes = [held([P, GROUPS, CHUNK], U32, f"h_codes{c}") for c in range(CHUNKS)]
         tab, w1_raw, w1_bf, w1_codes, w1_plane, w3_raw, w3, w4_plane = {}, {}, {}, {}, {}, {}, {}, {}
         v, h, h_bf, template, w4 = {}, {}, {}, {}, {}
@@ -102,10 +102,12 @@ def tile_list_sonar_template_misfit_kernel(
         def gather_planes():
             nc.vector.tensor_copy(picked[:], window[:].indirect(offsets[:]))
 
-        def gather(a, c, kib):
+        def gather(a, c, kib, pieces=1):
             v[a, c] = staged([P, CHUNK], U32, f"v{a}{c}", kib)
-            cols = CHUNK // 16
-            nc.vector.tensor_copy(v[a, c][:], tab[a][:].bitcast(U32).indirect(offsets[:, cols * c : cols * (c + 1)]))
+            step = CHUNK // pieces
+            for at in range(0, CHUNK, step):
+                cols = slice((CHUNK * c + at) // 16, (CHUNK * c + at + step) // 16)
+                nc.vector.tensor_copy(v[a, c][:, at : at + step], tab[a][:].bitcast(U32).indirect(offsets[:, cols]))
 
         def deal_w3_words(g, copy, kib):
             w3[g] = staged([P, PASSES, 2 * SPAN], U8, f"w3_{g}", kib)
@@ -143,17 +145,17 @@ def tile_list_sonar_template_misfit_kernel(
             c, at = divmod(lo, CHUNK)
             return v[a, c][:, at : at + hi - lo].bitcast(E4M3), v_plane[a][:, lo:hi]
 
-        def first_pass(acc, g, lo, hi, t, a):
+        def first_pass(acc, g, lo, hi, t, a, last=True):
             m = slice(P * t, P * (t + 1))
             nc.tensor.matmul_mx(
                 acc, w1_codes[g, a][:, m].bitcast(E4M3), w1_plane[g, a][:, m], *picked_operand(a, lo, hi),
-                start=(a == 0), stop=(a == PASSES - 1))
+                start=(a == 0), stop=(last and a == PASSES - 1))
 
-        def skip_pass(acc, g, lo, hi, t, a):
+        def skip_pass(acc, g, lo, hi, t, a, last=True):
             at = SPAN * g + P * t
             nc.tensor.matmul_mx(
                 acc, w3[g][:, a, 2 * P * t : 2 * P * (t + 1)].bitcast(E2M1), w3_plane[:, a, at : at + P],
-                *picked_operand(a, lo, hi), start=(a == 0), stop=(a == PASSES - 1))
+                *picked_operand(a, lo, hi), start=(a == 0), stop=(last and a == PASSES - 1))
 
         def combine(g, lo, hi, t, first, skip, kib=None):
             if g not in h:
@@ -187,23 +189,23 @@ def tile_list_sonar_template_misfit_kernel(
         def quantize_h(g, unit):
             lo, hi = unit
             nc.vector.quantize_mx(
-                h_codes[lo // CHUNK][:, g, :].bitcast(E4M3), h_plane[H_ROW:P, g, lo:hi], h_bf[g, unit][:])
+                h_codes[lo // CHUNK][:, g, :].bitcast(E4M3), h_plane[lo // CHUNK][H_ROW:P, g, :], h_bf[g, unit][:])
 
         def store_codes(c, g0, g1):
             words = out_2.rearrange("g p m t -> p g (m t)").bitcast(I32)
             nc.sync.dma_start(words[:, g0:g1, CHUNK * c : CHUNK * (c + 1)], h_codes[c][:, g0:g1].bitcast(I32))
 
-        def store_planes():
+        def store_planes(c):
             for r in range(QUADS):
                 nc.sync.dma_start(
-                    out_3[:, r::4, :].rearrange("g q m -> q g m").bitcast(I32),
-                    h_plane[H_ROW + r : P : 32].bitcast(I32))
+                    out_3[:, r::4, CHUNK * c : CHUNK * (c + 1)].rearrange("g q m -> q g m").bitcast(I32),
+                    h_plane[c][H_ROW + r : P : 32].bitcast(I32))
 
         def sig_pass(acc, b, lo, hi, g, start, stop):
             m = slice(P * b, P * (b + 1))
             nc.tensor.matmul_mx(
                 acc, w4[0][:, g, m].bitcast(E4M3), w4_plane[0][W4_ROW:P, g, m],
-                h_codes[lo // CHUNK][:, g, :].bitcast(E4M3), h_plane[H_ROW:P, g, lo:hi], start=start, stop=stop)
+                h_codes[lo // CHUNK][:, g, :].bitcast(E4M3), h_plane[lo // CHUNK][H_ROW:P, g, :], start=start, stop=stop)
 
         def misfit(acc, b0, b1, lo, hi, name=None):
             n = b1 - b0
@@ -237,8 +239,8 @@ def tile_list_sonar_template_misfit_kernel(
         load_w3()
         load_w1(0, 0, 48)
         gather_planes()
-        load_w1(0, 1, 15.5)
         spread(0)
+        load_w1(0, 1, 15.5)
         load_tab(1, 24)
         spread(1)
         load_gain()
@@ -262,8 +264,11 @@ def tile_list_sonar_template_misfit_kernel(
             first_pass(firsts[t], 0, 0, CHUNK, t, 0)
         for t in range(PACK):
             skip_pass(skips[t], 0, 0, CHUNK, t, 0)
-        gather(1, 0, 85)
-        for t in range(PACK):
+        gather(1, 0, 85, pieces=2)
+        for t, lo in ((0, 0), (1, 0), (0, 256), (1, 256)):
+            first_pass(firsts[t][:, lo : lo + 256], 0, lo, lo + 256, t, 1, last=lo > 0)
+            skip_pass(skips[t][:, lo : lo + 256], 0, lo, lo + 256, t, 1, last=lo > 0)
+        for t in (2, 3):
             first_pass(firsts[t], 0, 0, CHUNK, t, 1)
             skip_pass(skips[t], 0, 0, CHUNK, t, 1)
         gather(1, 1, 87)
@@ -295,10 +300,12 @@ def tile_list_sonar_template_misfit_kernel(
             if t % 2 == 1:
                 store_h(1, t - 1, t + 1, 0, CHUNK)
         quantize_h(0, low)
+        store_codes(0, 0, 1)
         round_h(1, low, 0, 192, on_s)
         round_h(1, low, 192, 512, on_v)
         quantize_h(1, low)
-        store_codes(0, 0, 2)
+        store_codes(0, 1, 2)
+        store_planes(0)
         slice_of_h(1, CHUNK, S, 0)
         slice_of_h(1, CHUNK, S, 1)
         store_h(1, 0, 2, CHUNK, S)
@@ -318,6 +325,7 @@ def tile_list_sonar_template_misfit_kernel(
         round_h(1, high, 0, 256, on_s)
         round_h(1, high, 256, 512, on_v)
         misfit(sigs[2], 2, 3, 0, CHUNK)
+        store_y(2, 3, 0, CHUNK)
         quantize_h(0, high)
         store_codes(1, 0, 1)
         quantize_h(1, high)
@@ -326,9 +334,9 @@ def tile_list_sonar_template_misfit_kernel(
             for b in range(N // P):
                 sig_pass(sigs[4 + b], b, CHUNK, S, g, g == 0, g == 1)
         misfit(sigs[3], 3, 4, 0, CHUNK)
-        store_y(2, 4, 0, CHUNK)
+        store_y(3, 4, 0, CHUNK)
         store_codes(1, 1, 2)
-        store_planes()
+        store_planes(1)
         for b in range(N // P):
             misfit(sigs[4 + b], b, b + 1, CHUNK, S)
             store_y(b, b + 1, CHUNK, S)

@@ -158,18 +158,22 @@ def tile_list_sonar_template_misfit_kernel(
                 *picked_operand(a, lo, hi), start=(a == 0), stop=(last and a == PASSES - 1))
 
         def combine(g, lo, hi, t, first, skip, kib=None):
-            if g not in h:
-                h[g] = held([P, PACK, S], F32, f"h{g}")
+            if g == 0 and g not in h:
+                h[g] = held([P, PACK, S], F32, "h0")
+                h[0, 0], h[0, CHUNK] = h[0][:, :, 0:CHUNK], h[0][:, :, CHUNK:S]
+            if (g, lo) not in h:
+                h[g, lo] = held([P, PACK, CHUNK], F32, f"h{g}{lo}")[:]
             if kib is None:
                 th = ring.tile([P, hi - lo], F32, name="th")
             else:
                 th = staged([P, hi - lo], F32, f"th{t}", kib)
             nc.scalar.activation(th[:], first, ACT.Tanh)
-            nc.vector.scalar_tensor_tensor(h[g][:, t, lo:hi], th[:], gain[:, g, t : t + 1], skip, ALU.mult, ALU.add)
+            nc.vector.scalar_tensor_tensor(h[g, lo][:, t, :], th[:], gain[:, g, t : t + 1], skip, ALU.mult, ALU.add)
 
         def store_h(g, t0, t1, lo, hi):
             rows = out_1[SPAN * g : SPAN * (g + 1), lo:hi].rearrange("(p t) j -> p t j", t=PACK)
-            nc.sync.dma_start(rows[:, t0:t1, :], h[g][:, t0:t1, lo:hi])
+            values = h[g][:] if hi - lo == S else h[g, lo]
+            nc.sync.dma_start(rows[:, t0:t1, :], values[:, t0:t1, :])
 
         def slice_of_h(g, lo, hi, t):
             first, skip = bank(2 * t)[:], bank(2 * t + 1)[:]
@@ -183,7 +187,7 @@ def tile_list_sonar_template_misfit_kernel(
             if (g, unit) not in h_bf:
                 h_bf[g, unit] = held([P, (unit[1] - unit[0]) * PACK], BF16, name or f"h_bf{g}{unit[0]}")
             dst = h_bf[g, unit][:].rearrange("p (b i t) -> p b t i", i=4, t=PACK)
-            src = h[g][:, :, unit[0] : unit[1]].rearrange("p t (b i) -> p b t i", i=4)
+            src = h[g, unit[0]].rearrange("p t (b i) -> p b t i", i=4)
             copy(dst[:, lo // 4 : hi // 4], src[:, lo // 4 : hi // 4])
 
         def quantize_h(g, unit):

from contextlib import ExitStack

import concourse.mybir as mybir

K, H, N, T, S = 1024, 1024, 512, 2048, 1024
FLOPS = 2 * (2 * K * H * S + H * N * S)

F32 = mybir.dt.float32
BF16 = mybir.dt.bfloat16
I32 = mybir.dt.int32
U32 = mybir.dt.uint32
U16 = mybir.dt.uint16
U8 = mybir.dt.uint8
E4M3 = mybir.dt.float8_e4m3fn_x4
E2M1 = mybir.dt.float4_e2m1fn_x4
ACT = mybir.ActivationFunctionType
ALU = mybir.AluOpType

P = 128
PACK = 4
SPAN = P * PACK
PASSES = K // SPAN
GROUPS = H // SPAN
CHUNK = 512
CHUNKS = S // CHUNK
QUADS = 4
ROWS = 16
H_ROW = 4
W4_ROW = 8


def tile_list_sonar_template_misfit_kernel(
    tc, tab_words, tab_scales, offs, w1, w2, w3_words, w3_scales, w4_words, w4_scales, tpl,
    out_0, out_1, out_2, out_3,
):
    nc = tc.nc
    with ExitStack() as ctx:
        keep = ctx.enter_context(tc.tile_pool(name="keep", bufs=1))
        ring = ctx.enter_context(tc.tile_pool(name="ring", bufs=4))
        psum = ctx.enter_context(tc.psum_pool(name="psum", bufs=1))
        stage = ctx.enter_context(tc.tile_pool(name="stage", bufs=1))

        def staged(shape, dtype, name, kib):
            return stage.tile(shape, dtype, name=name, align_bytes=64, offset=int(1024 * kib))

        def held(shape, dtype, name):
            return keep.tile(shape, dtype, name=name, align_bytes=64)

        offsets = keep.tile([P, S // 16], U16, name="offsets")
        window = staged([P, T], U8, "window", 23)
        w3_rows = held([P, PASSES, H], U8, "w3_rows")
        picked = held([P, S], U8, "picked")
        v_plane = [held([P, S], U8, f"v_plane{a}") for a in range(PASSES)]
        w3_plane = held([P, PASSES, H], U8, "w3_plane")
        gain = staged([P, GROUPS, PACK], F32, "gain", 23.5)
        h_plane = [held([P, GROUPS, CHUNK], U8, f"h_plane{c}") for c in range(CHUNKS)]
        h_codes = [held([P, GROUPS, CHUNK], U32, f"h_codes{c}") for c in range(CHUNKS)]
        tab, w1_raw, w1_bf, w1_codes, w1_plane, w3_raw, w3, w4_plane = {}, {}, {}, {}, {}, {}, {}, {}
        v, h, h_bf, template, w4 = {}, {}, {}, {}, {}
        y = held([P, N // P, S], F32, "y")

        def load_tab(a, kib):
            tab[a] = staged([P, T], I32, f"tab{a}", kib)
            nc.sync.dma_start(tab[a][:], tab_words[a].rearrange("p t i -> p (t i)").bitcast(I32))

        def load_rows(tile, scales):
            nc.sync.dma_start(tile[0 : PASSES * ROWS, :].bitcast(I32), scales.rearrange("a u n -> u a n").bitcast(I32))

        def spread(a):
            for q in (0, 2, 1, 3):
                nc.sync.dma_start(
                    v_plane[a][32 * q : 32 * q + 4, :].bitcast(I32), picked[8 * q + a : 8 * q + 8 : 2, :].bitcast(I32))

        def load_w3():
            w3_raw[0] = held([P, PASSES, 2 * H // 4], I32, "w3_raw")
            nc.sync.dma_start(w3_raw[0][:], w3_words.rearrange("a p n -> p a n").bitcast(I32))

        def load_gain():
            nc.sync.dma_start(gain[:], w2.rearrange("(g p t) -> p g t", p=P, t=PACK))

        def load_w1(g, a, kib):
            w1_raw[g, a] = staged([P, PACK, SPAN], F32, f"w1_raw{g}{a}", kib)
            rows = w1[SPAN * a : SPAN * (a + 1), SPAN * g : SPAN * (g + 1)]
            nc.sync.dma_start(w1_raw[g, a][:], rows.rearrange("(p i) c -> p i c", i=PACK))

        def load_template(u, kib):
            template[u] = staged([P, 2, S], F32, f"template{u}", kib)
            nc.sync.dma_start(template[u][:], tpl[2 * P * u : 2 * P * (u + 1), :].rearrange("(b p) j -> p b j", p=P))

        def load_w4(kib):
            w4[0] = staged([P, GROUPS, N], I32, "w4", kib)
            nc.sync.dma_start(w4[0][:], w4_words.rearrange("a p c i -> p a (c i)").bitcast(I32))

        def load_w4_scales(kib):
            w4_plane[0] = staged([P, GROUPS, N], U8, "w4_plane", kib)
            nc.vector.memset(w4_plane[0][:].rearrange("p a n -> p (a n)").bitcast(I32), 0)
            for r in range(QUADS):
                nc.sync.dma_start(
                    w4_plane[0][W4_ROW + r : P : 32].bitcast(I32),
                    w4_scales[:, r::4, :].rearrange("a q n -> q a n").bitcast(I32))

        def gather_planes():
            nc.vector.tensor_copy(picked[:], window[:].indirect(offsets[:]))

        def gather(a, c, kib, pieces=1):
            v[a, c] = staged([P, CHUNK], U32, f"v{a}{c}", kib)
            step = CHUNK // pieces
            for at in range(0, CHUNK, step):
                cols = slice((CHUNK * c + at) // 16, (CHUNK * c + at + step) // 16)
                nc.vector.tensor_copy(v[a, c][:, at : at + step], tab[a][:].bitcast(U32).indirect(offsets[:, cols]))

        def deal_w3_words(g, copy, kib):
            w3[g] = staged([P, PASSES, 2 * SPAN], U8, f"w3_{g}", kib)
            copy(
                w3[g][:].bitcast(U16).rearrange("p a (t m) -> p a t m", t=PACK),
                w3_raw[0][:].bitcast(U16)[:, :, SPAN * g : SPAN * (g + 1)].rearrange("p a (m t) -> p a t m", t=PACK))

        def load_w3_scales():
            for r in range(QUADS):
                nc.sync.dma_start(
                    w3_rows[r:P:32].bitcast(I32), w3_scales[:, r::4, :].rearrange("a q n -> q a n").bitcast(I32))

        def deal_w3_plane():
            nc.vector.tensor_copy(
                w3_plane[:].rearrange("p a (g t m) -> p (a g) t m", g=GROUPS, t=PACK),
                w3_rows[:].rearrange("p a (g m t) -> p (a g) t m", g=GROUPS, t=PACK))

        def round_w1(g, a, t0, t1, copy, kib):
            rounded = staged([P, (t1 - t0) * SPAN], BF16, f"w1_bf{g}{a}{t0}", kib)
            w1_bf[g, a, t0] = rounded
            dealt = rounded[:].rearrange("p (t m i) -> p m i t", t=t1 - t0, i=PACK)
            copy(dealt, w1_raw[g, a][:].rearrange("p i (m t) -> p m i t", t=PACK)[:, :, :, t0:t1])

        def quantize_w1(g, a, t0, t1):
            if (g, a) not in w1_codes:
                w1_codes[g, a] = held([P, SPAN], U32, f"w1_codes{g}{a}")
                w1_plane[g, a] = held([P, SPAN], U8, f"w1_plane{g}{a}")
            m = slice(P * t0, P * t1)
            nc.vector.quantize_mx(w1_codes[g, a][:, m].bitcast(E4M3), w1_plane[g, a][:, m], w1_bf[g, a, t0][:])

        def bank(n):
            return psum.tile([P, CHUNK], F32, name=f"bank{n}")

        def picked_operand(a, lo, hi):
            c, at = divmod(lo, CHUNK)
            return v[a, c][:, at : at + hi - lo].bitcast(E4M3), v_plane[a][:, lo:hi]

        def first_pass(acc, g, lo, hi, t, a, last=True):
            m = slice(P * t, P * (t + 1))
            nc.tensor.matmul_mx(
                acc, w1_codes[g, a][:, m].bitcast(E4M3), w1_plane[g, a][:, m], *picked_operand(a, lo, hi),
                start=(a == 0), stop=(last and a == PASSES - 1))

        def skip_pass(acc, g, lo, hi, t, a, last=True):
            at = SPAN * g + P * t
            nc.tensor.matmul_mx(
                acc, w3[g][:, a, 2 * P * t : 2 * P * (t + 1)].bitcast(E2M1), w3_plane[:, a, at : at + P],
                *picked_operand(a, lo, hi), start=(a == 0), stop=(last and a == PASSES - 1))

        def combine(g, lo, hi, t, first, skip, kib=None):
            if g == 0 and g not in h:
                h[g] = held([P, PACK, S], F32, "h0")
                h[0, 0], h[0, CHUNK] = h[0][:, :, 0:CHUNK], h[0][:, :, CHUNK:S]
            if (g, lo) not in h:
                h[g, lo] = held([P, PACK, CHUNK], F32, f"h{g}{lo}")[:]
            if kib is None:
                th = ring.tile([P, hi - lo], F32, name="th")
            else:
                th = staged([P, hi - lo], F32, f"th{t}", kib)
            nc.scalar.activation(th[:], first, ACT.Tanh)
            nc.vector.scalar_tensor_tensor(h[g, lo][:, t, :], th[:], gain[:, g, t : t + 1], skip, ALU.mult, ALU.add)

        def store_h(g, t0, t1, lo, hi):
            rows = out_1[SPAN * g : SPAN * (g + 1), lo:hi].rearrange("(p t) j -> p t j", t=PACK)
            values = h[g][:] if hi - lo == S else h[g, lo]
            nc.sync.dma_start(rows[:, t0:t1, :], values[:, t0:t1, :])

        def slice_of_h(g, lo, hi, t):
            first, skip = bank(2 * t)[:], bank(2 * t + 1)[:]
            for a in range(PASSES):
                first_pass(first, g, lo, hi, t, a)
            for a in range(PASSES):
                skip_pass(skip, g, lo, hi, t, a)
            combine(g, lo, hi, t, first, skip)

        def round_h(g, unit, lo, hi, copy, name=None):
            if (g, unit) not in h_bf:
                h_bf[g, unit] = held([P, (unit[1] - unit[0]) * PACK], BF16, name or f"h_bf{g}{unit[0]}")
            dst = h_bf[g, unit][:].rearrange("p (b i t) -> p b t i", i=4, t=PACK)
            src = h[g, unit[0]].rearrange("p t (b i) -> p b t i", i=4)
            copy(dst[:, lo // 4 : hi // 4], src[:, lo // 4 : hi // 4])

        def quantize_h(g, unit):
            lo, hi = unit
            nc.vector.quantize_mx(
                h_codes[lo // CHUNK][:, g, :].bitcast(E4M3), h_plane[lo // CHUNK][H_ROW:P, g, :], h_bf[g, unit][:])

        def store_codes(c, g0, g1):
            words = out_2.rearrange("g p m t -> p g (m t)").bitcast(I32)
            nc.sync.dma_start(words[:, g0:g1, CHUNK * c : CHUNK * (c + 1)], h_codes[c][:, g0:g1].bitcast(I32))

        def store_planes(c):
            for r in range(QUADS):
                nc.sync.dma_start(
                    out_3[:, r::4, CHUNK * c : CHUNK * (c + 1)].rearrange("g q m -> q g m").bitcast(I32),
                    h_plane[c][H_ROW + r : P : 32].bitcast(I32))

        def sig_pass(acc, b, lo, hi, g, start, stop):
            m = slice(P * b, P * (b + 1))
            nc.tensor.matmul_mx(
                acc, w4[0][:, g, m].bitcast(E4M3), w4_plane[0][W4_ROW:P, g, m],
                h_codes[lo // CHUNK][:, g, :].bitcast(E4M3), h_plane[lo // CHUNK][H_ROW:P, g, :], start=start, stop=stop)

        def misfit(acc, b0, b1, lo, hi, name=None):
            n = b1 - b0
            if name is None:
                diff = ring.tile([P, n, hi - lo], F32, name="diff")
            else:
                diff = held([P, n, hi - lo], F32, name)
            nc.vector.tensor_tensor(
                diff[:], template[b0 // 2][:, b0 % 2 : b0 % 2 + n, lo:hi],
                acc.rearrange("p (b j) -> p b j", b=n), ALU.subtract)
            nc.scalar.activation(y[:, b0:b1, lo:hi], diff[:], ACT.Square)

        def store_y(b0, b1, lo, hi):
            rows = out_0[:, lo:hi].rearrange("(b p) j -> p b j", p=P)
            nc.sync.dma_start(rows[:, b0:b1, :], y[:, b0:b1, lo:hi])

        on_v, on_s = nc.vector.tensor_copy, nc.scalar.copy

        def on_act(out, in_):
            nc.scalar.activation(out, in_, ACT.Copy)

        nc.vector.memset(w3_rows[:].rearrange("p a n -> p (a n)").bitcast(I32), 0)
        nc.vector.memset(window[32:64, :].bitcast(I32), 0)
        nc.vector.memset(window[64:P, :].bitcast(I32), 0)
        for a in range(PASSES):
            nc.vector.memset(v_plane[a][:].bitcast(I32), 0)
        load_rows(window, tab_scales)
        nc.sync.dma_start(offsets[:], offs)
        load_tab(0, 64)
        load_w3_scales()
        load_w3()
        load_w1(0, 0, 48)
        gather_planes()
        spread(0)
        load_w1(0, 1, 15.5)
        load_tab(1, 24)
        spread(1)
        load_gain()
        gather(0, 0, 90)
        deal_w3_plane()
        gather(0, 1, 92)
        deal_w3_words(1, on_s, 80)
        pairs = [(bank(2 * t)[:], bank(2 * t + 1)[:]) for t in range(PACK)]
        firsts = [pair[0] for pair in pairs]
        skips = [pair[1] for pair in pairs]
        for a in range(PASSES):
            round_w1(0, a, 0, 2, on_v, 84)
            round_w1(0, a, 2, 4, on_act, 86)
            quantize_w1(0, a, 0, 2)
            quantize_w1(0, a, 2, 4)
            if a == 0:
                deal_w3_words(0, on_s, 54)
        load_w1(1, 0, 60)
        load_w1(1, 1, 68)
        for t in range(PACK):
            first_pass(firsts[t], 0, 0, CHUNK, t, 0)
        for t in range(PACK):
            skip_pass(skips[t], 0, 0, CHUNK, t, 0)
        gather(1, 0, 85, pieces=2)
        for t, lo in ((0, 0), (1, 0), (0, 256), (1, 256)):
            first_pass(firsts[t][:, lo : lo + 256], 0, lo, lo + 256, t, 1, last=lo > 0)
            skip_pass(skips[t][:, lo : lo + 256], 0, lo, lo + 256, t, 1, last=lo > 0)
        for t in (2, 3):
            first_pass(firsts[t], 0, 0, CHUNK, t, 1)
            skip_pass(skips[t], 0, 0, CHUNK, t, 1)
        gather(1, 1, 87)
        load_w4(48)
        load_w4_scales(52)
        load_template(0, 8)
        load_template(1, 28)
        combine(0, 0, CHUNK, 0, firsts[0], skips[0], 100)
        round_w1(1, 0, 0, 2, on_v, 99)
        combine(0, 0, CHUNK, 1, firsts[1], skips[1], 104)
        quantize_w1(1, 0, 0, 2)
        combine(0, 0, CHUNK, 2, firsts[2], skips[2], 106)
        round_w1(1, 0, 2, 4, on_s, 101)
        combine(0, 0, CHUNK, 3, firsts[3], skips[3])
        round_w1(1, 1, 0, 2, on_v, 106)
        round_w1(1, 1, 2, 4, on_s, 104)
        quantize_w1(1, 0, 2, 4)
        slice_of_h(0, CHUNK, S, 0)
        quantize_w1(1, 1, 0, 2)
        quantize_w1(1, 1, 2, 4)
        for t in range(1, PACK):
            slice_of_h(0, CHUNK, S, t)
            if t % 2 == 1:
                store_h(0, t - 1, t + 1, 0, S)
        low, high = (0, CHUNK), (CHUNK, S)
        for t in range(PACK):
            round_h(0, low, P * t, P * (t + 1), on_s if t < 2 else on_v)
            slice_of_h(1, 0, CHUNK, t)
            if t % 2 == 1:
                store_h(1, t - 1, t + 1, 0, CHUNK)
        quantize_h(0, low)
        store_codes(0, 0, 1)
        round_h(1, low, 0, 192, on_s)
        round_h(1, low, 192, 512, on_v)
        quantize_h(1, low)
        store_codes(0, 1, 2)
        store_planes(0)
        slice_of_h(1, CHUNK, S, 0)
        slice_of_h(1, CHUNK, S, 1)
        store_h(1, 0, 2, CHUNK, S)
        slice_of_h(1, CHUNK, S, 2)
        for t in range(PACK):
            round_h(0, high, P * t, P * (t + 1), on_s if t < 3 else on_v)
        sigs = [bank(b)[:] for b in range(N // P)]
        for b in range(N // P):
            for g in range(GROUPS):
                sig_pass(sigs[b], b, 0, CHUNK, g, g == 0, g == 1)
            if b < 2:
                misfit(sigs[b], b, b + 1, 0, CHUNK)
                store_y(b, b + 1, 0, CHUNK)
            if b == 1:
                slice_of_h(1, CHUNK, S, 3)
                store_h(1, 2, 4, CHUNK, S)
        round_h(1, high, 0, 256, on_s)
        round_h(1, high, 256, 512, on_v)
        misfit(sigs[2], 2, 3, 0, CHUNK)
        store_y(2, 3, 0, CHUNK)
        quantize_h(0, high)
        store_codes(1, 0, 1)
        quantize_h(1, high)
        sigs += [bank(4 + b)[:] for b in range(N // P)]
        for g in range(GROUPS):
            for b in range(N // P):
                sig_pass(sigs[4 + b], b, CHUNK, S, g, g == 0, g == 1)
        misfit(sigs[3], 3, 4, 0, CHUNK)
        store_y(3, 4, 0, CHUNK)
        store_codes(1, 1, 2)
        store_planes(1)
        for b in range(N // P):
            misfit(sigs[4 + b], b, b + 1, CHUNK, S)
            store_y(b, b + 1, CHUNK, S)
